import numpy as np
import ml_dtypes


def mxq(x, axis, fmt="e4m3"):
    dtype, down = {"e4m3": (ml_dtypes.float8_e4m3fn, 7), "e5m2": (ml_dtypes.float8_e5m2, 14)}[fmt]
    v = np.moveaxis(np.asarray(x, np.float32).astype(ml_dtypes.bfloat16).astype(np.float64), axis, -1)
    blocks = v.reshape(v.shape[:-1] + (-1, 32))
    amax = np.abs(blocks).max(-1, keepdims=True)
    byte = np.maximum(np.where(amax > 0, np.frexp(amax)[1] - 1 + 127, 0) - down, 1)
    scale = np.exp2(byte - 127.0)
    codes = (blocks / scale).astype(np.float32).astype(dtype).astype(np.float64)
    return np.moveaxis((codes * scale).reshape(v.shape), -1, axis)


WIDE = False


def mx_kscale(k):
    if not WIDE:
        return np.ones(k)
    levels = np.array([10, -10, 5, -5, 0])
    if k % 512:
        return np.exp2(np.random.permutation(np.resize(levels, k // 32))).repeat(32)
    a = np.empty((k // 512, 16))
    for p in range(k // 512):
        a[p, :8] = np.random.permutation(np.resize(levels, 8))
        for g in range(8):
            far = levels[np.abs(levels - a[p, g]) >= 10]
            a[p, g + 8] = far[np.random.randint(len(far))]
    return np.exp2(a.ravel()).repeat(32)


def f64(x):
    return np.asarray(x).astype(np.float64)


def striped(idx):
    return np.tile(np.asarray(idx).reshape(-1, 16).T, (8, 1)).astype(np.uint16)


def unstriped(offs):
    return offs[:16].T.reshape(-1).astype(np.int64)


E2M1 = np.array([0.0, 0.5, 1.0, 1.5, 2.0, 3.0, 4.0, 6.0, -0.0, -0.5, -1.0, -1.5, -2.0, -3.0, -4.0, -6.0])


def pack_weight(w, fmt):
    k, n = w.shape
    w = f64(np.asarray(w, np.float32).astype(ml_dtypes.bfloat16)).reshape(k // 32, 32, n)
    amax = np.abs(w).max(1)
    if fmt == "e4m3":
        byte = np.frexp(amax)[1] - 1 + 127 - 7
    else:
        mant, ex = np.frexp(amax / 6.0)
        byte = np.where(mant > 0.5, ex, ex - 1) + 127
    byte = np.clip(np.where(amax > 0, byte, 1), 1, 254)
    scaled = (w * np.exp2(127.0 - byte)[:, None, :]).reshape(k, n).astype(np.float32)
    by_word = np.ascontiguousarray(scaled.reshape(k // 512, 128, 4, n).transpose(0, 1, 3, 2))
    if fmt == "e4m3":
        words = by_word.astype(ml_dtypes.float8_e4m3fn).view(np.uint8)
    else:
        c = by_word.astype(ml_dtypes.float4_e2m1fn).view(np.uint8) & 0xF
        words = (c[..., 0::2] | (c[..., 1::2] << 4)).reshape(k // 512, 128, 2 * n)
    return np.ascontiguousarray(words), np.ascontiguousarray(byte.astype(np.uint8).reshape(k // 512, 16, n))


def unpack_weight(words, scales, fmt):
    g, _, n = scales.shape
    words = np.ascontiguousarray(words).reshape(g, 128, n, -1)
    if fmt == "e4m3":
        vals = words.view(ml_dtypes.float8_e4m3fn).astype(np.float64)
    else:
        nib = np.empty((g, 128, n, 4), np.uint8)
        nib[..., 0::2] = words & 0xF
        nib[..., 1::2] = words >> 4
        vals = E2M1[nib]
    vals = vals * np.repeat(np.exp2(scales.astype(np.float64) - 127.0), 8, axis=1)[..., None]
    return vals.transpose(0, 1, 3, 2).reshape(g * 512, n)


def bf(x):
    return np.asarray(x, np.float32).astype(ml_dtypes.bfloat16)


def planes(Y):
    r, m = Y.shape
    b = f64(bf(Y)).reshape(r // 32, 32, m)
    amax = np.abs(b).max(1)
    byte = np.clip(np.where(amax > 0, np.frexp(amax)[1] - 1 + 127 - 7, 1), 1, 254)
    codes = (b * np.exp2(127.0 - byte)[:, None, :]).reshape(r, m).astype(np.float32).astype(ml_dtypes.float8_e4m3fn).view(np.uint8)
    words = codes.reshape(r // 512, 128, 4, m).transpose(0, 1, 3, 2)
    return np.ascontiguousarray(words), np.ascontiguousarray(byte.astype(np.uint8).reshape(r // 512, 16, m))


B, N, T, D, NQ = 1, 512, 2048, 512, 512


def setup_inputs():
    n = np.random.standard_normal
    idx = np.random.permutation(T)[:B * N]
    s = mx_kscale(D)[:, None]
    kp = pack_weight(n((D, T)) / s, "e4m3")
    cp = pack_weight(n((D, T)) / s, "e4m3")
    return {
        "qT": (n((B, D, NQ)) * s * (0.40 / np.sqrt(D))).astype(np.float32),
        "k_words": kp[0],
        "k_scales": kp[1],
        "c_words": cp[0],
        "c_scales": cp[1],
        "ls": (np.random.uniform(7.8, 8.4, (B, 1, NQ))).astype(np.float32),
        "offs": striped(idx),
    }


def reference(qT, k_words, k_scales, c_words, c_scales, ls, offs):
    idx = unstriped(offs)
    pick = lambda x, which: x[:, which].reshape(x.shape[0], B, -1).transpose(1, 0, 2)
    k = unpack_weight(k_words, k_scales, "e4m3")
    kg = pick(k, idx)
    c = unpack_weight(c_words, c_scales, "e4m3")
    cg = pick(c, idx)
    qq = mxq(f64(qT), 1, "e4m3")
    a = kg.transpose(0, 2, 1) @ qq
    z = cg.transpose(0, 2, 1) @ qq
    y = np.exp(1.5 * a - 0.5 * z - f64(ls))
    Y = y[0]
    words, scales = planes(Y)
    return Y, words, scales

@@ -1,0 +1,143 @@
+from contextlib import ExitStack
+
+import concourse.mybir as mybir
+from concourse.masks import make_identity
+
+F32 = mybir.dt.float32
+BF16 = mybir.dt.bfloat16
+I32 = mybir.dt.int32
+U32 = mybir.dt.uint32
+U16 = mybir.dt.uint16
+U8 = mybir.dt.uint8
+FP8X4 = mybir.dt.float8_e4m3fn_x4
+ALU = mybir.AluOpType
+ACT = mybir.ActivationFunctionType
+
+P = 128
+PACK = 4
+SLOTS, TOKENS, D, NQ = 512, 2048, 512, 512
+QT = NQ // P
+C_ROW = 4
+
+FLOPS = 2 * 2 * SLOTS * D * NQ
+
+
+def tile_attend_plw_cfg_topk_kernel(tc, qT, k_words, k_scales, c_words, c_scales, ls, offs, out_0, out_1, out_2):
+    nc = tc.nc
+    with ExitStack() as ctx:
+        keep = ctx.enter_context(tc.tile_pool(name="keep", bufs=1))
+        psum = ctx.enter_context(tc.psum_pool(name="psum", bufs=1))
+
+        offsets = keep.tile([P, SLOTS // 16], U16, name="offsets")
+        k_pool = keep.tile([P, TOKENS], U32, name="k_pool", align_bytes=64)
+        c_pool = keep.tile([P, TOKENS], U32, name="c_pool", align_bytes=64)
+        ks_pool = keep.tile([P, TOKENS], U8, name="ks_pool", tag="k_bytes", align_bytes=64)
+        cs_pool = keep.tile([P, TOKENS], U8, name="cs_pool", tag="c_bytes", align_bytes=64)
+        ls_rows = keep.tile([P, P], F32, name="ls_rows")
+        warm_in = keep.tile([P, 1], F32, name="warm_in")
+        warm_out = keep.tile([P, 1], F32, name="warm_out")
+        ident = keep.tile([P, P], F32, name="ident")
+        q_raw = [keep.tile([P, PACK, NQ // 2], F32, name="q_raw%d" % h) for h in range(2)]
+
+        nc.sync.dma_start(offsets[:], offs)
+        nc.sync.dma_start(k_pool[:].bitcast(I32), k_words[0].rearrange("p n t -> p (n t)").bitcast(I32))
+        q_rows = qT[0].rearrange("(p j) w -> p j w", j=PACK)
+        for h in range(2):
+            nc.sync.dma_start(q_raw[h][:], q_rows[:, :, h * 256:(h + 1) * 256])
+        nc.sync.dma_start(c_pool[:].bitcast(I32), c_words[0].rearrange("p n t -> p (n t)").bitcast(I32))
+
+        nc.vector.memset(ks_pool[:].bitcast(I32), 0)
+        nc.vector.memset(cs_pool[:].bitcast(I32), 0)
+        nc.vector.memset(warm_in[:], 0.0)
+        nc.vector.memset(ls_rows[:], 0.0)
+        make_identity(nc, ident[:])
+        for quad in range(4):
+            eng = nc.gpsimd if quad == 3 else nc.scalar
+            eng.dma_start(ks_pool[32 * quad:32 * quad + 4, :].bitcast(I32), k_scales[0, 4 * quad:4 * quad + 4, :].bitcast(I32))
+        for quad in range(4):
+            nc.gpsimd.dma_start(cs_pool[32 * quad + C_ROW:32 * quad + C_ROW + 4, :].bitcast(I32),
+                                c_scales[0, 4 * quad:4 * quad + 4, :].bitcast(I32))
+        nc.scalar.activation(warm_out[:], warm_in[:], ACT.Exp)
+        nc.scalar.dma_start(ls_rows[0:QT, :], ls[0, 0].rearrange("(t p) -> t p", p=P))
+
+        kg = keep.tile([P, SLOTS], U32, name="kg", tag="k_bytes", align_bytes=64)
+        ksg = keep.tile([P, SLOTS], U8, name="ksg", align_bytes=64)
+        cg = keep.tile([P, SLOTS], U32, name="cg", tag="c_bytes", align_bytes=64)
+        csg = keep.tile([P, SLOTS], U8, name="csg", align_bytes=64)
+        nc.vector.tensor_copy(ksg[:], ks_pool[:].indirect(offsets[:]))
+        nc.vector.tensor_copy(kg[:], k_pool[:].indirect(offsets[:]))
+
+        ls_ps = psum.tile([P, P], F32, name="ls_ps", tag="bank7")
+        nc.tensor.transpose(ls_ps[:], ls_rows[:], ident[:])
+        neg_ls = keep.tile([P, QT], F32, name="neg_ls")
+        nc.scalar.activation(neg_ls[:], ls_ps[:, 0:QT], ACT.Copy, scale=-1.0)
+
+        q_codes, q_scales = [], []
+        for h in range(2):
+            q_bf = keep.tile([P, NQ // 2, PACK], BF16, name="q_bf%d" % h, align_bytes=64)
+            dst = q_bf[:].rearrange("p (c i) t -> p c t i", i=4)
+            src = q_raw[h][:].rearrange("p t (c i) -> p c t i", i=4)
+            if h == 0:
+                nc.scalar.copy(dst, src)
+            else:
+                nc.vector.tensor_copy(dst, src)
+            codes = keep.tile([P, NQ // 2], U32, name="q_codes%d" % h, align_bytes=64)
+            scales = keep.tile([P, NQ // 2], U8, name="q_scales%d" % h, align_bytes=64)
+            nc.vector.quantize_mx(out=codes[:].bitcast(FP8X4), scales=scales[:], in_=q_bf[:].rearrange("p w j -> p (w j)"))
+            q_codes.append(codes)
+            q_scales.append(scales)
+
+        def scores(bank, t, words, plane):
+            cols = slice((t % 2) * P, (t % 2 + 1) * P)
+            nc.tensor.matmul_mx(out=bank[:], lhsT=q_codes[t // 2][:, cols].bitcast(FP8X4), lhsT_scale=q_scales[t // 2][:, cols],
+                                rhs=words[:].bitcast(FP8X4), rhs_scale=plane, start=True, stop=True)
+
+        def dealt(bank):
+            return bank[:].rearrange("p (s r) -> p r s", r=PACK)
+
+        u = []
+        for t in range(QT):
+            a_ps = psum.tile([P, SLOTS], F32, name="a_ps%d" % t, tag="bank%d" % t)
+            scores(a_ps, t, kg, ksg[:])
+            u_t = keep.tile([P, PACK, P], F32, name="u%d" % t)
+            nc.scalar.activation(u_t[:], dealt(a_ps), ACT.Identity, bias=neg_ls[:, t:t + 1], scale=1.5)
+            u.append(u_t)
+
+        nc.vector.tensor_copy(csg[:], cs_pool[:].indirect(offsets[:]))
+        nc.vector.tensor_copy(cg[:], c_pool[:].indirect(offsets[:]))
+
+        y_rows = out_0.rearrange("(p r) q -> p r q", r=PACK)
+        y_words = out_1[0].rearrange("p n t -> p (n t)").bitcast(I32)
+        y_codes = keep.tile([P, NQ], U32, name="y_codes", align_bytes=64)
+        y_scales = keep.tile([P, NQ], U8, name="y_scales", align_bytes=64)
+        z = []
+        for t in range(QT):
+            z_ps = psum.tile([P, SLOTS], F32, name="z_ps%d" % t, tag="bank%d" % (QT + t))
+            scores(z_ps, t, cg, csg[C_ROW:P, :])
+            z.append(z_ps)
+        y = []
+        for t in range(QT):
+            w_t = keep.tile([P, PACK, P], F32, name="w%d" % t)
+            nc.vector.scalar_tensor_tensor(w_t[:], dealt(z[t]), -0.5, u[t][:], ALU.mult, ALU.add)
+            wT = psum.tile([P, PACK, P], F32, name="wT%d" % t, tag="bank%d" % t)
+            for r in range(PACK):
+                nc.tensor.transpose(wT[:, r, :], w_t[:, r, :], ident[:])
+            y_t = keep.tile([P, PACK, P], F32, name="y%d" % t)
+            nc.scalar.activation(y_t[:], wT[:], ACT.Exp)
+            nc.sync.dma_start(y_rows[:, :, t * P:(t + 1) * P], y_t[:])
+            y.append(y_t)
+        y_bf = []
+        for t in range(QT):
+            b_t = keep.tile([P, P, PACK], BF16, name="y_bf%d" % t, align_bytes=64)
+            nc.vector.tensor_copy(b_t[:].rearrange("p (c i) t -> p c t i", i=4), y[t][:].rearrange("p t (c i) -> p c t i", i=4))
+            y_bf.append(b_t)
+            if t % 2 == 1:
+                for s in (t - 1, t):
+                    cols = slice(s * P, (s + 1) * P)
+                    nc.vector.quantize_mx(out=y_codes[:, cols].bitcast(FP8X4), scales=y_scales[:, cols],
+                                          in_=y_bf[s][:].rearrange("p w j -> p (w j)"))
+                cols = slice((t - 1) * P, (t + 1) * P)
+                nc.sync.dma_start(y_words[:, cols], y_codes[:, cols].bitcast(I32))
+        for quad in range(4):
+            eng = nc.sync if quad == 0 else nc.scalar
+            eng.dma_start(out_2[0, 4 * quad:4 * quad + 4, :].bitcast(I32), y_scales[32 * quad:32 * quad + 4, :].bitcast(I32))

@@ -29,63 +29,49 @@ def tile_attend_plw_cfg_topk_kernel(tc, qT, k_words, k_scales, c_words, c_scales
         psum = ctx.enter_context(tc.psum_pool(name="psum", bufs=1))
 
         offsets = keep.tile([P, SLOTS // 16], U16, name="offsets")
-        k_pool = keep.tile([P, TOKENS], U32, name="k_pool", align_bytes=64)
-        c_pool = keep.tile([P, TOKENS], U32, name="c_pool", align_bytes=64)
-        ks_pool = keep.tile([P, TOKENS], U8, name="ks_pool", tag="k_bytes", align_bytes=64)
-        cs_pool = keep.tile([P, TOKENS], U8, name="cs_pool", tag="c_bytes", align_bytes=64)
+        ks_pool = keep.tile([P, TOKENS], U8, name="ks_pool", align_bytes=64)
+        cs_pool = keep.tile([P, TOKENS], U8, name="cs_pool", align_bytes=64)
         ls_rows = keep.tile([P, P], F32, name="ls_rows")
         warm_in = keep.tile([P, 1], F32, name="warm_in")
         warm_out = keep.tile([P, 1], F32, name="warm_out")
         ident = keep.tile([P, P], F32, name="ident")
-        q_raw = [keep.tile([P, PACK, NQ // 2], F32, name="q_raw%d" % h) for h in range(2)]
+        q_raw = keep.tile([P, PACK, NQ], F32, name="q_raw")
+
+        k_pool = keep.tile([P, TOKENS], U32, name="k_pool", align_bytes=64)
+        c_pool = keep.tile([P, TOKENS], U32, name="c_pool", align_bytes=64)
+
+        nc.gpsimd.memset(ls_rows[:], 0.0)
+        nc.vector.memset(ks_pool[:].bitcast(I32), 0)
+        nc.vector.memset(warm_in[:], 0.0)
+        nc.vector.memset(cs_pool[:].bitcast(I32), 0)
+        make_identity(nc, ident[:])
 
         nc.sync.dma_start(offsets[:], offs)
+        nc.sync.dma_start(ls_rows[0:QT, :], ls[0, 0].rearrange("(t p) -> t p", p=P))
+        for j in range(4):
+            eng = nc.scalar if j < 2 else nc.sync
+            eng.dma_start(ks_pool[j:P:32, :].bitcast(I32), k_scales[0, j:16:4, :].bitcast(I32))
+        nc.sync.dma_start(q_raw[:], qT[0].rearrange("(p j) w -> p j w", j=PACK))
+        for j in range(4):
+            eng = nc.scalar if j < 2 else nc.sync
+            eng.dma_start(cs_pool[C_ROW + j:P:32, :].bitcast(I32), c_scales[0, j:16:4, :].bitcast(I32))
         nc.sync.dma_start(k_pool[:].bitcast(I32), k_words[0].rearrange("p n t -> p (n t)").bitcast(I32))
-        q_rows = qT[0].rearrange("(p j) w -> p j w", j=PACK)
-        for h in range(2):
-            nc.sync.dma_start(q_raw[h][:], q_rows[:, :, h * 256:(h + 1) * 256])
         nc.sync.dma_start(c_pool[:].bitcast(I32), c_words[0].rearrange("p n t -> p (n t)").bitcast(I32))
-
-        nc.vector.memset(ks_pool[:].bitcast(I32), 0)
-        nc.vector.memset(cs_pool[:].bitcast(I32), 0)
-        nc.vector.memset(warm_in[:], 0.0)
-        nc.vector.memset(ls_rows[:], 0.0)
-        make_identity(nc, ident[:])
-        for quad in range(4):
-            eng = nc.gpsimd if quad == 3 else nc.scalar
-            eng.dma_start(ks_pool[32 * quad:32 * quad + 4, :].bitcast(I32), k_scales[0, 4 * quad:4 * quad + 4, :].bitcast(I32))
-        for quad in range(4):
-            nc.gpsimd.dma_start(cs_pool[32 * quad + C_ROW:32 * quad + C_ROW + 4, :].bitcast(I32),
-                                c_scales[0, 4 * quad:4 * quad + 4, :].bitcast(I32))
         nc.scalar.activation(warm_out[:], warm_in[:], ACT.Exp)
-        nc.scalar.dma_start(ls_rows[0:QT, :], ls[0, 0].rearrange("(t p) -> t p", p=P))
-
-        kg = keep.tile([P, SLOTS], U32, name="kg", tag="k_bytes", align_bytes=64)
-        ksg = keep.tile([P, SLOTS], U8, name="ksg", align_bytes=64)
-        cg = keep.tile([P, SLOTS], U32, name="cg", tag="c_bytes", align_bytes=64)
-        csg = keep.tile([P, SLOTS], U8, name="csg", align_bytes=64)
-        nc.vector.tensor_copy(ksg[:], ks_pool[:].indirect(offsets[:]))
-        nc.vector.tensor_copy(kg[:], k_pool[:].indirect(offsets[:]))
 
         ls_ps = psum.tile([P, P], F32, name="ls_ps", tag="bank7")
         nc.tensor.transpose(ls_ps[:], ls_rows[:], ident[:])
         neg_ls = keep.tile([P, QT], F32, name="neg_ls")
         nc.scalar.activation(neg_ls[:], ls_ps[:, 0:QT], ACT.Copy, scale=-1.0)
 
-        q_codes, q_scales = [], []
-        for h in range(2):
-            q_bf = keep.tile([P, NQ // 2, PACK], BF16, name="q_bf%d" % h, align_bytes=64)
-            dst = q_bf[:].rearrange("p (c i) t -> p c t i", i=4)
-            src = q_raw[h][:].rearrange("p t (c i) -> p c t i", i=4)
-            if h == 0:
-                nc.scalar.copy(dst, src)
-            else:
-                nc.vector.tensor_copy(dst, src)
-            codes = keep.tile([P, NQ // 2], U32, name="q_codes%d" % h, align_bytes=64)
-            scales = keep.tile([P, NQ // 2], U8, name="q_scales%d" % h, align_bytes=64)
-            nc.vector.quantize_mx(out=codes[:].bitcast(FP8X4), scales=scales[:], in_=q_bf[:].rearrange("p w j -> p (w j)"))
-            q_codes.append(codes)
-            q_scales.append(scales)
+        ksg = keep.tile([P, SLOTS], U8, name="ksg", align_bytes=64)
+        kg = keep.tile([P, SLOTS], U32, name="kg", align_bytes=64)
+        csg = keep.tile([P, SLOTS], U8, name="csg", align_bytes=64)
+        cg = keep.tile([P, SLOTS], U32, name="cg", align_bytes=64)
+        nc.vector.tensor_copy(ksg[:], ks_pool[:].indirect(offsets[:]))
+        nc.vector.tensor_copy(csg[:], cs_pool[:].indirect(offsets[:]))
+
+        q_codes, q_scales, u = [], [], []
 
         def scores(bank, t, words, plane):
             cols = slice((t % 2) * P, (t % 2 + 1) * P)
@@ -95,15 +81,30 @@ def tile_attend_plw_cfg_topk_kernel(tc, qT, k_words, k_scales, c_words, c_scales
         def dealt(bank):
             return bank[:].rearrange("p (s r) -> p r s", r=PACK)
 
-        u = []
+        q_bf = []
+        for h in range(2):
+            b_h = keep.tile([P, NQ // 2, PACK], BF16, name="q_bf%d" % h, align_bytes=64)
+            nc.scalar.copy(b_h[:].rearrange("p (c i) t -> p c t i", i=4),
+                           q_raw[:, :, h * 256:(h + 1) * 256].rearrange("p t (c i) -> p c t i", i=4))
+            q_bf.append(b_h)
+        for h in range(2):
+            if h == 1:
+                nc.vector.tensor_copy(kg[:], k_pool[:].indirect(offsets[:]))
+            codes = keep.tile([P, NQ // 2], U32, name="q_codes%d" % h, align_bytes=64)
+            scales = keep.tile([P, NQ // 2], U8, name="q_scales%d" % h, align_bytes=64)
+            nc.vector.quantize_mx(out=codes[:].bitcast(FP8X4), scales=scales[:], in_=q_bf[h][:].rearrange("p w j -> p (w j)"))
+            q_codes.append(codes)
+            q_scales.append(scales)
+        for t in range(QT):
+            warm_ps = psum.tile([P, NQ // 2], F32, name="warm_ps%d" % t, tag="bank%d" % t)
+            nc.tensor.matmul_mx(out=warm_ps[:], lhsT=q_codes[0][:, 0:P].bitcast(FP8X4), lhsT_scale=q_scales[0][:, 0:P],
+                                rhs=q_codes[0][:].bitcast(FP8X4), rhs_scale=q_scales[0][:], start=True, stop=True)
         for t in range(QT):
             a_ps = psum.tile([P, SLOTS], F32, name="a_ps%d" % t, tag="bank%d" % t)
             scores(a_ps, t, kg, ksg[:])
             u_t = keep.tile([P, PACK, P], F32, name="u%d" % t)
             nc.scalar.activation(u_t[:], dealt(a_ps), ACT.Identity, bias=neg_ls[:, t:t + 1], scale=1.5)
             u.append(u_t)
-
-        nc.vector.tensor_copy(csg[:], cs_pool[:].indirect(offsets[:]))
         nc.vector.tensor_copy(cg[:], c_pool[:].indirect(offsets[:]))
 
         y_rows = out_0.rearrange("(p r) q -> p r q", r=PACK)
@@ -115,29 +116,41 @@ def tile_attend_plw_cfg_topk_kernel(tc, qT, k_words, k_scales, c_words, c_scales
             z_ps = psum.tile([P, SLOTS], F32, name="z_ps%d" % t, tag="bank%d" % (QT + t))
             scores(z_ps, t, cg, csg[C_ROW:P, :])
             z.append(z_ps)
-        y = []
+        y_first = keep.tile([P, PACK, P], F32, name="y_first")
+        y_mid = keep.tile([P, PACK, 2 * P], F32, name="y_mid")
+        y_last = keep.tile([P, PACK, P], F32, name="y_last")
+        y = [y_first[:], y_mid[:, :, 0:P], y_mid[:, :, P:2 * P], y_last[:]]
+        stores = {0: (y_first, 0, P), 2: (y_mid, P, 3 * P), 3: (y_last, 3 * P, NQ)}
+        y_bf = [keep.tile([P, P, PACK], BF16, name="y_bf%d" % t, align_bytes=64) for t in range(QT)]
         for t in range(QT):
             w_t = keep.tile([P, PACK, P], F32, name="w%d" % t)
             nc.vector.scalar_tensor_tensor(w_t[:], dealt(z[t]), -0.5, u[t][:], ALU.mult, ALU.add)
             wT = psum.tile([P, PACK, P], F32, name="wT%d" % t, tag="bank%d" % t)
             for r in range(PACK):
                 nc.tensor.transpose(wT[:, r, :], w_t[:, r, :], ident[:])
-            y_t = keep.tile([P, PACK, P], F32, name="y%d" % t)
-            nc.scalar.activation(y_t[:], wT[:], ACT.Exp)
-            nc.sync.dma_start(y_rows[:, :, t * P:(t + 1) * P], y_t[:])
-            y.append(y_t)
-        y_bf = []
-        for t in range(QT):
-            b_t = keep.tile([P, P, PACK], BF16, name="y_bf%d" % t, align_bytes=64)
-            nc.vector.tensor_copy(b_t[:].rearrange("p (c i) t -> p c t i", i=4), y[t][:].rearrange("p t (c i) -> p c t i", i=4))
-            y_bf.append(b_t)
+            if t == QT - 1:
+                nc.scalar.activation(y_bf[t][:], wT[:].rearrange("p r q -> p q r"), ACT.Exp)
+            nc.scalar.activation(y[t], wT[:], ACT.Exp)
+            if t in stores:
+                tile, lo, hi = stores[t]
+                nc.sync.dma_start(y_rows[:, :, lo:hi], tile[:])
+
+        def interleave(t):
+            nc.vector.tensor_copy(y_bf[t][:].rearrange("p (c i) t -> p c t i", i=4), y[t].rearrange("p t (c i) -> p c t i", i=4))
+
+        def quantise(t):
+            cols = slice(t * P, (t + 1) * P)
+            nc.vector.quantize_mx(out=y_codes[:, cols].bitcast(FP8X4), scales=y_scales[:, cols],
+                                  in_=y_bf[t][:].rearrange("p w j -> p (w j)"))
             if t % 2 == 1:
-                for s in (t - 1, t):
-                    cols = slice(s * P, (s + 1) * P)
-                    nc.vector.quantize_mx(out=y_codes[:, cols].bitcast(FP8X4), scales=y_scales[:, cols],
-                                          in_=y_bf[s][:].rearrange("p w j -> p (w j)"))
                 cols = slice((t - 1) * P, (t + 1) * P)
                 nc.sync.dma_start(y_words[:, cols], y_codes[:, cols].bitcast(I32))
-        for quad in range(4):
-            eng = nc.sync if quad == 0 else nc.scalar
-            eng.dma_start(out_2[0, 4 * quad:4 * quad + 4, :].bitcast(I32), y_scales[32 * quad:32 * quad + 4, :].bitcast(I32))
+
+        interleave(0)
+        for t in range(QT):
+            if t + 1 < QT - 1:
+                interleave(t + 1)
+            quantise(t)
+        for j in range(4):
+            eng = nc.sync if j == 0 else nc.scalar
+            eng.dma_start(out_2[0, j:16:4, :].bitcast(I32), y_scales[j:P:32, :].bitcast(I32))

@@ -15,15 +15,26 @@ ACT = mybir.ActivationFunctionType
 
 P = 128
 PACK = 4
+QUAD = 32
+ROWS = 4
 SLOTS, TOKENS, D, NQ = 512, 2048, 512, 512
 QT = NQ // P
+HALF = NQ // 2
 C_ROW = 4
+LINE = 4
 
 FLOPS = 2 * 2 * SLOTS * D * NQ
 
 
 def tile_attend_plw_cfg_topk_kernel(tc, qT, k_words, k_scales, c_words, c_scales, ls, offs, out_0, out_1, out_2):
     nc = tc.nc
+
+    def woven(dst, src):
+        return dst.rearrange("p (c i) t -> p c t i", i=LINE), src.rearrange("p t (c i) -> p c t i", i=LINE)
+
+    def as_words(packed):
+        return packed[0].rearrange("p n t -> p (n t)").bitcast(I32)
+
     with ExitStack() as ctx:
         keep = ctx.enter_context(tc.tile_pool(name="keep", bufs=1))
         psum = ctx.enter_context(tc.psum_pool(name="psum", bufs=1))
@@ -32,34 +43,29 @@ def tile_attend_plw_cfg_topk_kernel(tc, qT, k_words, k_scales, c_words, c_scales
         ks_pool = keep.tile([P, TOKENS], U8, name="ks_pool", align_bytes=64)
         cs_pool = keep.tile([P, TOKENS], U8, name="cs_pool", align_bytes=64)
         ls_rows = keep.tile([P, P], F32, name="ls_rows")
-        warm_in = keep.tile([P, 1], F32, name="warm_in")
-        warm_out = keep.tile([P, 1], F32, name="warm_out")
         ident = keep.tile([P, P], F32, name="ident")
         q_raw = keep.tile([P, PACK, NQ], F32, name="q_raw")
-
         k_pool = keep.tile([P, TOKENS], U32, name="k_pool", align_bytes=64)
         c_pool = keep.tile([P, TOKENS], U32, name="c_pool", align_bytes=64)
 
         nc.gpsimd.memset(ls_rows[:], 0.0)
         nc.vector.memset(ks_pool[:].bitcast(I32), 0)
-        nc.vector.memset(warm_in[:], 0.0)
         nc.vector.memset(cs_pool[:].bitcast(I32), 0)
         make_identity(nc, ident[:])
 
         nc.sync.dma_start(offsets[:], offs)
         nc.sync.dma_start(ls_rows[0:QT, :], ls[0, 0].rearrange("(t p) -> t p", p=P))
-        for j in range(4):
-            eng = nc.scalar if j < 2 else nc.sync
-            eng.dma_start(ks_pool[j:P:32, :].bitcast(I32), k_scales[0, j:16:4, :].bitcast(I32))
+        for j in range(ROWS):
+            queue = nc.scalar if j < ROWS // 2 else nc.sync
+            queue.dma_start(ks_pool[j:P:QUAD, :].bitcast(I32), k_scales[0, j:ROWS * ROWS:ROWS, :].bitcast(I32))
         nc.sync.dma_start(q_raw[:], qT[0].rearrange("(p j) w -> p j w", j=PACK))
-        for j in range(4):
-            eng = nc.scalar if j < 2 else nc.sync
-            eng.dma_start(cs_pool[C_ROW + j:P:32, :].bitcast(I32), c_scales[0, j:16:4, :].bitcast(I32))
-        nc.sync.dma_start(k_pool[:].bitcast(I32), k_words[0].rearrange("p n t -> p (n t)").bitcast(I32))
-        nc.sync.dma_start(c_pool[:].bitcast(I32), c_words[0].rearrange("p n t -> p (n t)").bitcast(I32))
-        nc.scalar.activation(warm_out[:], warm_in[:], ACT.Exp)
+        for j in range(ROWS):
+            queue = nc.scalar if j < ROWS // 2 else nc.sync
+            queue.dma_start(cs_pool[C_ROW + j:P:QUAD, :].bitcast(I32), c_scales[0, j:ROWS * ROWS:ROWS, :].bitcast(I32))
+        nc.sync.dma_start(k_pool[:].bitcast(I32), as_words(k_words))
+        nc.sync.dma_start(c_pool[:].bitcast(I32), as_words(c_words))
 
-        ls_ps = psum.tile([P, P], F32, name="ls_ps", tag="bank7")
+        ls_ps = psum.tile([P, P], F32, name="ls_ps", tag="bank%d" % (2 * QT - 1))
         nc.tensor.transpose(ls_ps[:], ls_rows[:], ident[:])
         neg_ls = keep.tile([P, QT], F32, name="neg_ls")
         nc.scalar.activation(neg_ls[:], ls_ps[:, 0:QT], ACT.Copy, scale=-1.0)
@@ -71,34 +77,34 @@ def tile_attend_plw_cfg_topk_kernel(tc, qT, k_words, k_scales, c_words, c_scales
         nc.vector.tensor_copy(ksg[:], ks_pool[:].indirect(offsets[:]))
         nc.vector.tensor_copy(csg[:], cs_pool[:].indirect(offsets[:]))
 
-        q_codes, q_scales, u = [], [], []
+        q_bf = []
+        for h in range(2):
+            rounded = keep.tile([P, HALF, PACK], BF16, name="q_bf%d" % h, align_bytes=64)
+            nc.scalar.copy(*woven(rounded[:], q_raw[:, :, h * HALF:(h + 1) * HALF]))
+            q_bf.append(rounded)
 
-        def scores(bank, t, words, plane):
+        q_codes, q_scales = [], []
+
+        def quantise_q(h):
+            codes = keep.tile([P, HALF], U32, name="q_codes%d" % h, align_bytes=64)
+            scales = keep.tile([P, HALF], U8, name="q_scales%d" % h, align_bytes=64)
+            nc.vector.quantize_mx(out=codes[:].bitcast(FP8X4), scales=scales[:], in_=q_bf[h][:].rearrange("p w j -> p (w j)"))
+            q_codes.append(codes)
+            q_scales.append(scales)
+
+        quantise_q(0)
+        nc.vector.tensor_copy(kg[:], k_pool[:].indirect(offsets[:]))
+        quantise_q(1)
+
+        def scores(bank, t, words, scale_rows):
             cols = slice((t % 2) * P, (t % 2 + 1) * P)
             nc.tensor.matmul_mx(out=bank[:], lhsT=q_codes[t // 2][:, cols].bitcast(FP8X4), lhsT_scale=q_scales[t // 2][:, cols],
-                                rhs=words[:].bitcast(FP8X4), rhs_scale=plane, start=True, stop=True)
+                                rhs=words[:].bitcast(FP8X4), rhs_scale=scale_rows, start=True, stop=True)
 
         def dealt(bank):
             return bank[:].rearrange("p (s r) -> p r s", r=PACK)
 
-        q_bf = []
-        for h in range(2):
-            b_h = keep.tile([P, NQ // 2, PACK], BF16, name="q_bf%d" % h, align_bytes=64)
-            nc.scalar.copy(b_h[:].rearrange("p (c i) t -> p c t i", i=4),
-                           q_raw[:, :, h * 256:(h + 1) * 256].rearrange("p t (c i) -> p c t i", i=4))
-            q_bf.append(b_h)
-        for h in range(2):
-            if h == 1:
-                nc.vector.tensor_copy(kg[:], k_pool[:].indirect(offsets[:]))
-            codes = keep.tile([P, NQ // 2], U32, name="q_codes%d" % h, align_bytes=64)
-            scales = keep.tile([P, NQ // 2], U8, name="q_scales%d" % h, align_bytes=64)
-            nc.vector.quantize_mx(out=codes[:].bitcast(FP8X4), scales=scales[:], in_=q_bf[h][:].rearrange("p w j -> p (w j)"))
-            q_codes.append(codes)
-            q_scales.append(scales)
-        for t in range(QT):
-            warm_ps = psum.tile([P, NQ // 2], F32, name="warm_ps%d" % t, tag="bank%d" % t)
-            nc.tensor.matmul_mx(out=warm_ps[:], lhsT=q_codes[0][:, 0:P].bitcast(FP8X4), lhsT_scale=q_scales[0][:, 0:P],
-                                rhs=q_codes[0][:].bitcast(FP8X4), rhs_scale=q_scales[0][:], start=True, stop=True)
+        u = []
         for t in range(QT):
             a_ps = psum.tile([P, SLOTS], F32, name="a_ps%d" % t, tag="bank%d" % t)
             scores(a_ps, t, kg, ksg[:])
@@ -108,7 +114,7 @@ def tile_attend_plw_cfg_topk_kernel(tc, qT, k_words, k_scales, c_words, c_scales
         nc.vector.tensor_copy(cg[:], c_pool[:].indirect(offsets[:]))
 
         y_rows = out_0.rearrange("(p r) q -> p r q", r=PACK)
-        y_words = out_1[0].rearrange("p n t -> p (n t)").bitcast(I32)
+        y_words = as_words(out_1)
         y_codes = keep.tile([P, NQ], U32, name="y_codes", align_bytes=64)
         y_scales = keep.tile([P, NQ], U8, name="y_scales", align_bytes=64)
         z = []
@@ -116,41 +122,36 @@ def tile_attend_plw_cfg_topk_kernel(tc, qT, k_words, k_scales, c_words, c_scales
             z_ps = psum.tile([P, SLOTS], F32, name="z_ps%d" % t, tag="bank%d" % (QT + t))
             scores(z_ps, t, cg, csg[C_ROW:P, :])
             z.append(z_ps)
-        y_first = keep.tile([P, PACK, P], F32, name="y_first")
-        y_mid = keep.tile([P, PACK, 2 * P], F32, name="y_mid")
-        y_last = keep.tile([P, PACK, P], F32, name="y_last")
-        y = [y_first[:], y_mid[:, :, 0:P], y_mid[:, :, P:2 * P], y_last[:]]
-        stores = {0: (y_first, 0, P), 2: (y_mid, P, 3 * P), 3: (y_last, 3 * P, NQ)}
+
+        y = [keep.tile([P, PACK, P], F32, name="y%d" % t) for t in range(QT)]
         y_bf = [keep.tile([P, P, PACK], BF16, name="y_bf%d" % t, align_bytes=64) for t in range(QT)]
         for t in range(QT):
             w_t = keep.tile([P, PACK, P], F32, name="w%d" % t)
             nc.vector.scalar_tensor_tensor(w_t[:], dealt(z[t]), -0.5, u[t][:], ALU.mult, ALU.add)
-            wT = psum.tile([P, PACK, P], F32, name="wT%d" % t, tag="bank%d" % t)
+            turned = psum.tile([P, PACK, P], F32, name="turned%d" % t, tag="bank%d" % t)
             for r in range(PACK):
-                nc.tensor.transpose(wT[:, r, :], w_t[:, r, :], ident[:])
+                nc.tensor.transpose(turned[:, r, :], w_t[:, r, :], ident[:])
             if t == QT - 1:
-                nc.scalar.activation(y_bf[t][:], wT[:].rearrange("p r q -> p q r"), ACT.Exp)
-            nc.scalar.activation(y[t], wT[:], ACT.Exp)
-            if t in stores:
-                tile, lo, hi = stores[t]
-                nc.sync.dma_start(y_rows[:, :, lo:hi], tile[:])
+                nc.scalar.activation(y_bf[t][:], turned[:].rearrange("p r q -> p q r"), ACT.Exp)
+            nc.scalar.activation(y[t][:], turned[:], ACT.Exp)
+            nc.sync.dma_start(y_rows[:, :, t * P:(t + 1) * P], y[t][:])
 
-        def interleave(t):
-            nc.vector.tensor_copy(y_bf[t][:].rearrange("p (c i) t -> p c t i", i=4), y[t].rearrange("p t (c i) -> p c t i", i=4))
+        def round_y(t):
+            nc.vector.tensor_copy(*woven(y_bf[t][:], y[t][:]))
 
-        def quantise(t):
+        def quantise_y(t):
             cols = slice(t * P, (t + 1) * P)
             nc.vector.quantize_mx(out=y_codes[:, cols].bitcast(FP8X4), scales=y_scales[:, cols],
                                   in_=y_bf[t][:].rearrange("p w j -> p (w j)"))
             if t % 2 == 1:
-                cols = slice((t - 1) * P, (t + 1) * P)
-                nc.sync.dma_start(y_words[:, cols], y_codes[:, cols].bitcast(I32))
+                pair = slice((t - 1) * P, (t + 1) * P)
+                nc.sync.dma_start(y_words[:, pair], y_codes[:, pair].bitcast(I32))
 
-        interleave(0)
+        round_y(0)
         for t in range(QT):
             if t + 1 < QT - 1:
-                interleave(t + 1)
-            quantise(t)
-        for j in range(4):
-            eng = nc.sync if j == 0 else nc.scalar
-            eng.dma_start(out_2[0, j:16:4, :].bitcast(I32), y_scales[j:P:32, :].bitcast(I32))
+                round_y(t + 1)
+            quantise_y(t)
+        for j in range(ROWS):
+            queue = nc.sync if j == 0 else nc.scalar
+            queue.dma_start(out_2[0, j:ROWS * ROWS:ROWS, :].bitcast(I32), y_scales[j:P:QUAD, :].bitcast(I32))

@@ -71,9 +71,9 @@ def tile_attend_plw_cfg_topk_kernel(tc, qT, k_words, k_scales, c_words, c_scales
         nc.scalar.activation(neg_ls[:], ls_ps[:, 0:QT], ACT.Copy, scale=-1.0)
 
         ksg = keep.tile([P, SLOTS], U8, name="ksg", align_bytes=64)
-        kg = keep.tile([P, SLOTS], U32, name="kg", align_bytes=64)
+        kg = [keep.tile([P, HALF], U32, name="kg%d" % h, align_bytes=64) for h in range(2)]
         csg = keep.tile([P, SLOTS], U8, name="csg", align_bytes=64)
-        cg = keep.tile([P, SLOTS], U32, name="cg", align_bytes=64)
+        cg = [keep.tile([P, HALF], U32, name="cg%d" % h, align_bytes=64) for h in range(2)]
         nc.vector.tensor_copy(ksg[:], ks_pool[:].indirect(offsets[:]))
         nc.vector.tensor_copy(csg[:], cs_pool[:].indirect(offsets[:]))
 
@@ -92,66 +92,76 @@ def tile_attend_plw_cfg_topk_kernel(tc, qT, k_words, k_scales, c_words, c_scales
             q_codes.append(codes)
             q_scales.append(scales)
 
-        quantise_q(0)
-        nc.vector.tensor_copy(kg[:], k_pool[:].indirect(offsets[:]))
-        quantise_q(1)
+        def gather_words(dst, pool, h):
+            nc.vector.tensor_copy(dst[h][:], pool[:].indirect(offsets[:, h * (HALF // 16):(h + 1) * (HALF // 16)]))
 
-        def scores(bank, t, words, scale_rows):
+        quantise_q(0)
+        quantise_q(1)
+        gather_words(kg, k_pool, 0)
+        gather_words(kg, k_pool, 1)
+
+        def scores(out, t, h, words, scales, first_row):
             cols = slice((t % 2) * P, (t % 2 + 1) * P)
-            nc.tensor.matmul_mx(out=bank[:], lhsT=q_codes[t // 2][:, cols].bitcast(FP8X4), lhsT_scale=q_scales[t // 2][:, cols],
-                                rhs=words[:].bitcast(FP8X4), rhs_scale=scale_rows, start=True, stop=True)
+            slots = slice(h * HALF, (h + 1) * HALF)
+            nc.tensor.matmul_mx(out=out, lhsT=q_codes[t // 2][:, cols].bitcast(FP8X4), lhsT_scale=q_scales[t // 2][:, cols],
+                                rhs=words[h][:].bitcast(FP8X4), rhs_scale=scales[first_row:P, slots], start=True, stop=True)
 
         def dealt(bank):
-            return bank[:].rearrange("p (s r) -> p r s", r=PACK)
+            return bank.rearrange("p (s r) -> p r s", r=PACK)
 
-        u = []
-        for t in range(QT):
-            a_ps = psum.tile([P, SLOTS], F32, name="a_ps%d" % t, tag="bank%d" % t)
-            scores(a_ps, t, kg, ksg[:])
-            u_t = keep.tile([P, PACK, P], F32, name="u%d" % t)
-            nc.scalar.activation(u_t[:], dealt(a_ps), ACT.Identity, bias=neg_ls[:, t:t + 1], scale=1.5)
-            u.append(u_t)
-        nc.vector.tensor_copy(cg[:], c_pool[:].indirect(offsets[:]))
+        a = [psum.tile([P, SLOTS], F32, name="a_ps%d" % t, tag="bank%d" % t) for t in range(QT)]
+        u = [keep.tile([P, PACK, 2, P], F32, name="u%d" % g) for g in range(2)]
+        w = [keep.tile([P, PACK, 2, P], F32, name="w%d" % g) for g in range(2)]
+        for g in range(2):
+            for h in range(2):
+                for t in range(2 * g, 2 * g + 2):
+                    scores(a[t][:, h * HALF:(h + 1) * HALF], t, h, kg, ksg, 0)
+            for t in range(2 * g, 2 * g + 2):
+                nc.scalar.activation(u[g][:, :, t % 2, :], dealt(a[t][:]), ACT.Identity, bias=neg_ls[:, t:t + 1], scale=1.5)
+        gather_words(cg, c_pool, 0)
+        gather_words(cg, c_pool, 1)
 
         y_rows = out_0.rearrange("(p r) q -> p r q", r=PACK)
         y_words = as_words(out_1)
         y_codes = keep.tile([P, NQ], U32, name="y_codes", align_bytes=64)
         y_scales = keep.tile([P, NQ], U8, name="y_scales", align_bytes=64)
-        z = []
-        for t in range(QT):
-            z_ps = psum.tile([P, SLOTS], F32, name="z_ps%d" % t, tag="bank%d" % (QT + t))
-            scores(z_ps, t, cg, csg[C_ROW:P, :])
-            z.append(z_ps)
 
-        y = [keep.tile([P, PACK, P], F32, name="y%d" % t) for t in range(QT)]
-        y_bf = [keep.tile([P, P, PACK], BF16, name="y_bf%d" % t, align_bytes=64) for t in range(QT)]
-        for t in range(QT):
-            w_t = keep.tile([P, PACK, P], F32, name="w%d" % t)
-            nc.vector.scalar_tensor_tensor(w_t[:], dealt(z[t]), -0.5, u[t][:], ALU.mult, ALU.add)
-            turned = psum.tile([P, PACK, P], F32, name="turned%d" % t, tag="bank%d" % t)
-            for r in range(PACK):
-                nc.tensor.transpose(turned[:, r, :], w_t[:, r, :], ident[:])
-            if t == QT - 1:
-                nc.scalar.activation(y_bf[t][:], turned[:].rearrange("p r q -> p q r"), ACT.Exp)
-            nc.scalar.activation(y[t][:], turned[:], ACT.Exp)
-            nc.sync.dma_start(y_rows[:, :, t * P:(t + 1) * P], y[t][:])
+        def half_of(pair, h):
+            return pair[:].rearrange("p r t (h s) -> p (r t) h s", h=2)[:, :, h, :]
 
-        def round_y(t):
-            nc.vector.tensor_copy(*woven(y_bf[t][:], y[t][:]))
+        for g in range(2):
+            for h in range(2):
+                z_ps = psum.tile([P, 2, HALF], F32, name="z_ps%d%d" % (g, h), tag="bank%d" % (QT + 2 * g + h))
+                for t in range(2):
+                    scores(z_ps[:, t, :], 2 * g + t, h, cg, csg, C_ROW)
+                parts = 2 if (g, h) == (0, 1) else 1
+                for part in range(parts):
+                    places = slice(part * PACK // parts, (part + 1) * PACK // parts)
+                    rows = slice(2 * places.start, 2 * places.stop)
+                    nc.vector.scalar_tensor_tensor(half_of(w[g], h)[:, rows, :], dealt(z_ps[:].rearrange("p t n -> p (t n)"))[:, places, :],
+                                                   -0.5, half_of(u[g], h)[:, rows, :], ALU.mult, ALU.add)
 
-        def quantise_y(t):
-            cols = slice(t * P, (t + 1) * P)
+        y = [keep.tile([P, PACK, HALF], F32, name="y%d" % g) for g in range(2)]
+        y_bf = [keep.tile([P, HALF, PACK], BF16, name="y_bf%d" % g, align_bytes=64) for g in range(2)]
+        pieces = [(0, 0, 1), (0, 1, 2), (0, 2, 4), (1, 0, 2), (1, 2, 4)]
+        for bank, (g, first, last) in enumerate(pieces):
+            turned = psum.tile([P, last - first, 2, P], F32, name="turned%d" % bank, tag="bank%d" % ((bank - 1) % (QT + 1)))
+            for r in range(first, last):
+                for t in range(2):
+                    nc.tensor.transpose(turned[:, r - first, t, :], w[g][:, r, t, :], ident[:])
+            nc.scalar.activation(y[g][:, first:last, :], turned[:].rearrange("p r t q -> p r (t q)"), ACT.Exp)
+            nc.sync.dma_start(y_rows[:, first:last, g * HALF:(g + 1) * HALF], y[g][:, first:last, :])
+
+        for g in range(2):
+            if g == 0:
+                nc.vector.tensor_copy(*woven(y_bf[g][:], y[g][:]))
+            else:
+                nc.vector.tensor_copy(*woven(y_bf[g][:, 0:P, :], y[g][:, :, 0:P]))
+                nc.scalar.copy(*woven(y_bf[g][:, P:HALF, :], y[g][:, :, P:HALF]))
+            cols = slice(g * HALF, (g + 1) * HALF)
             nc.vector.quantize_mx(out=y_codes[:, cols].bitcast(FP8X4), scales=y_scales[:, cols],
-                                  in_=y_bf[t][:].rearrange("p w j -> p (w j)"))
-            if t % 2 == 1:
-                pair = slice((t - 1) * P, (t + 1) * P)
-                nc.sync.dma_start(y_words[:, pair], y_codes[:, pair].bitcast(I32))
-
-        round_y(0)
-        for t in range(QT):
-            if t + 1 < QT - 1:
-                round_y(t + 1)
-            quantise_y(t)
+                                  in_=y_bf[g][:].rearrange("p w j -> p (w j)"))
+            nc.sync.dma_start(y_words[:, cols], y_codes[:, cols].bitcast(I32))
         for j in range(ROWS):
             queue = nc.sync if j == 0 else nc.scalar
             queue.dma_start(out_2[0, j:ROWS * ROWS:ROWS, :].bitcast(I32), y_scales[j:P:QUAD, :].bitcast(I32))

@@ -53,16 +53,14 @@ def tile_attend_plw_cfg_topk_kernel(tc, qT, k_words, k_scales, c_words, c_scales
         nc.vector.memset(cs_pool[:].bitcast(I32), 0)
         make_identity(nc, ident[:])
 
+        nc.sync.dma_start(q_raw[:], qT[0].rearrange("(p j) w -> p j w", j=PACK))
         nc.sync.dma_start(offsets[:], offs)
         nc.sync.dma_start(ls_rows[0:QT, :], ls[0, 0].rearrange("(t p) -> t p", p=P))
         for j in range(ROWS):
-            queue = nc.scalar if j < ROWS // 2 else nc.sync
-            queue.dma_start(ks_pool[j:P:QUAD, :].bitcast(I32), k_scales[0, j:ROWS * ROWS:ROWS, :].bitcast(I32))
-        nc.sync.dma_start(q_raw[:], qT[0].rearrange("(p j) w -> p j w", j=PACK))
-        for j in range(ROWS):
-            queue = nc.scalar if j < ROWS // 2 else nc.sync
-            queue.dma_start(cs_pool[C_ROW + j:P:QUAD, :].bitcast(I32), c_scales[0, j:ROWS * ROWS:ROWS, :].bitcast(I32))
+            nc.sync.dma_start(ks_pool[j:P:QUAD, :].bitcast(I32), k_scales[0, j:ROWS * ROWS:ROWS, :].bitcast(I32))
         nc.sync.dma_start(k_pool[:].bitcast(I32), as_words(k_words))
+        for j in range(ROWS):
+            nc.sync.dma_start(cs_pool[C_ROW + j:P:QUAD, :].bitcast(I32), c_scales[0, j:ROWS * ROWS:ROWS, :].bitcast(I32))
         nc.sync.dma_start(c_pool[:].bitcast(I32), as_words(c_words))
 
         ls_ps = psum.tile([P, P], F32, name="ls_ps", tag="bank%d" % (2 * QT - 1))
@@ -72,23 +70,26 @@ def tile_attend_plw_cfg_topk_kernel(tc, qT, k_words, k_scales, c_words, c_scales
 
         ksg = keep.tile([P, SLOTS], U8, name="ksg", align_bytes=64)
         kg = [keep.tile([P, HALF], U32, name="kg%d" % h, align_bytes=64) for h in range(2)]
-        csg = keep.tile([P, SLOTS], U8, name="csg", align_bytes=64)
         cg = [keep.tile([P, HALF], U32, name="cg%d" % h, align_bytes=64) for h in range(2)]
         nc.vector.tensor_copy(ksg[:], ks_pool[:].indirect(offsets[:]))
-        nc.vector.tensor_copy(csg[:], cs_pool[:].indirect(offsets[:]))
 
         q_bf = []
         for h in range(2):
             rounded = keep.tile([P, HALF, PACK], BF16, name="q_bf%d" % h, align_bytes=64)
-            nc.scalar.copy(*woven(rounded[:], q_raw[:, :, h * HALF:(h + 1) * HALF]))
+            if h == 0:
+                nc.scalar.copy(*woven(rounded[:], q_raw[:, :, 0:HALF]))
+            else:
+                nc.scalar.copy(*woven(rounded[:, 0:P, :], q_raw[:, :, HALF:HALF + P]))
+                nc.vector.tensor_copy(*woven(rounded[:, P:HALF, :], q_raw[:, :, HALF + P:NQ]))
             q_bf.append(rounded)
 
         q_codes, q_scales = [], []
+        all_codes = keep.tile([P, NQ], U32, name="q_codes", tag="ks_pool", align_bytes=64)
 
         def quantise_q(h):
-            codes = keep.tile([P, HALF], U32, name="q_codes%d" % h, align_bytes=64)
+            codes = all_codes[:, h * HALF:(h + 1) * HALF]
             scales = keep.tile([P, HALF], U8, name="q_scales%d" % h, align_bytes=64)
-            nc.vector.quantize_mx(out=codes[:].bitcast(FP8X4), scales=scales[:], in_=q_bf[h][:].rearrange("p w j -> p (w j)"))
+            nc.vector.quantize_mx(out=codes.bitcast(FP8X4), scales=scales[:], in_=q_bf[h][:].rearrange("p w j -> p (w j)"))
             q_codes.append(codes)
             q_scales.append(scales)
 
@@ -99,6 +100,8 @@ def tile_attend_plw_cfg_topk_kernel(tc, qT, k_words, k_scales, c_words, c_scales
         quantise_q(1)
         gather_words(kg, k_pool, 0)
         gather_words(kg, k_pool, 1)
+        csg = keep.tile([P, SLOTS], U8, name="csg", tag="k_pool", align_bytes=64)
+        nc.vector.tensor_copy(csg[:], cs_pool[:].indirect(offsets[:]))
 
         def scores(out, t, h, words, scales, first_row):
             cols = slice((t % 2) * P, (t % 2 + 1) * P)
@@ -108,6 +111,11 @@ def tile_attend_plw_cfg_topk_kernel(tc, qT, k_words, k_scales, c_words, c_scales
 
         def dealt(bank):
             return bank.rearrange("p (s r) -> p r s", r=PACK)
+
+        warm = psum.tile([P, HALF], F32, name="warm", tag="bank%d" % (2 * QT - 2))
+        for repeat in range(3):
+            nc.tensor.matmul_mx(out=warm[:], lhsT=q_codes[1][:, 0:P].bitcast(FP8X4), lhsT_scale=q_scales[1][:, 0:P],
+                                rhs=q_codes[1].bitcast(FP8X4), rhs_scale=q_scales[1][:], start=True, stop=True)
 
         a = [psum.tile([P, SLOTS], F32, name="a_ps%d" % t, tag="bank%d" % t) for t in range(QT)]
         u = [keep.tile([P, PACK, 2, P], F32, name="u%d" % g) for g in range(2)]
@@ -129,38 +137,41 @@ def tile_attend_plw_cfg_topk_kernel(tc, qT, k_words, k_scales, c_words, c_scales
         def half_of(pair, h):
             return pair[:].rearrange("p r t (h s) -> p (r t) h s", h=2)[:, :, h, :]
 
-        for g in range(2):
+        z_half = [psum.tile([P, 2, HALF], F32, name="z_half%d" % h, tag="bank%d" % (QT + h)) for h in range(2)]
+        z_tile = [psum.tile([P, SLOTS], F32, name="z_tile%d" % t, tag="bank%d" % (QT + 2 + t)) for t in range(2)]
+        for h in range(2):
+            for t in range(2):
+                scores(z_half[h][:, t, :], t, h, cg, csg, C_ROW)
+        for t in range(2):
             for h in range(2):
-                z_ps = psum.tile([P, 2, HALF], F32, name="z_ps%d%d" % (g, h), tag="bank%d" % (QT + 2 * g + h))
-                for t in range(2):
-                    scores(z_ps[:, t, :], 2 * g + t, h, cg, csg, C_ROW)
-                parts = 2 if (g, h) == (0, 1) else 1
-                for part in range(parts):
-                    places = slice(part * PACK // parts, (part + 1) * PACK // parts)
-                    rows = slice(2 * places.start, 2 * places.stop)
-                    nc.vector.scalar_tensor_tensor(half_of(w[g], h)[:, rows, :], dealt(z_ps[:].rearrange("p t n -> p (t n)"))[:, places, :],
-                                                   -0.5, half_of(u[g], h)[:, rows, :], ALU.mult, ALU.add)
+                scores(z_tile[t][:, h * HALF:(h + 1) * HALF], 2 + t, h, cg, csg, C_ROW)
 
-        y = [keep.tile([P, PACK, HALF], F32, name="y%d" % g) for g in range(2)]
-        y_bf = [keep.tile([P, HALF, PACK], BF16, name="y_bf%d" % g, align_bytes=64) for g in range(2)]
-        pieces = [(0, 0, 1), (0, 1, 2), (0, 2, 4), (1, 0, 2), (1, 2, 4)]
-        for bank, (g, first, last) in enumerate(pieces):
-            turned = psum.tile([P, last - first, 2, P], F32, name="turned%d" % bank, tag="bank%d" % ((bank - 1) % (QT + 1)))
-            for r in range(first, last):
-                for t in range(2):
-                    nc.tensor.transpose(turned[:, r - first, t, :], w[g][:, r, t, :], ident[:])
-            nc.scalar.activation(y[g][:, first:last, :], turned[:].rearrange("p r t q -> p r (t q)"), ACT.Exp)
-            nc.sync.dma_start(y_rows[:, first:last, g * HALF:(g + 1) * HALF], y[g][:, first:last, :])
+        def exponent(out, z, u_part):
+            nc.vector.scalar_tensor_tensor(out, dealt(z), -0.5, u_part, ALU.mult, ALU.add)
+
+        exponent(half_of(w[0], 0), z_half[0][:].rearrange("p t n -> p (t n)"), half_of(u[0], 0))
+        for t in range(2):
+            exponent(w[0][:, :, t, P // 2:P], z_half[1][:, t, :], u[0][:, :, t, P // 2:P])
+        for t in range(2):
+            exponent(w[1][:, :, t, :], z_tile[t][:], u[1][:, :, t, :])
+
+        y = [keep.tile([P, PACK, P], F32, name="y%d" % t) for t in range(QT)]
+        y_bf = keep.tile([P, NQ, PACK], BF16, name="y_bf", align_bytes=64)
+        for t in range(QT):
+            turned = psum.tile([P, PACK, P], F32, name="turned%d" % t, tag="bank%d" % t)
+            for r in range(PACK):
+                nc.tensor.transpose(turned[:, r, :], w[t // 2][:, r, t % 2, :], ident[:])
+            if t == QT - 1:
+                nc.scalar.activation(y_bf[:, t * P:(t + 1) * P, :], turned[:].rearrange("p r q -> p q r"), ACT.Exp)
+            nc.scalar.activation(y[t][:], turned[:], ACT.Exp)
+            nc.sync.dma_start(y_rows[:, :, t * P:(t + 1) * P], y[t][:])
 
         for g in range(2):
-            if g == 0:
-                nc.vector.tensor_copy(*woven(y_bf[g][:], y[g][:]))
-            else:
-                nc.vector.tensor_copy(*woven(y_bf[g][:, 0:P, :], y[g][:, :, 0:P]))
-                nc.scalar.copy(*woven(y_bf[g][:, P:HALF, :], y[g][:, :, P:HALF]))
+            for t in range(2 * g, min(2 * g + 2, QT - 1)):
+                nc.vector.tensor_copy(*woven(y_bf[:, t * P:(t + 1) * P, :], y[t][:]))
             cols = slice(g * HALF, (g + 1) * HALF)
             nc.vector.quantize_mx(out=y_codes[:, cols].bitcast(FP8X4), scales=y_scales[:, cols],
-                                  in_=y_bf[g][:].rearrange("p w j -> p (w j)"))
+                                  in_=y_bf[:, cols, :].rearrange("p w j -> p (w j)"))
             nc.sync.dma_start(y_words[:, cols], y_codes[:, cols].bitcast(I32))
         for j in range(ROWS):
             queue = nc.sync if j == 0 else nc.scalar

@@ -55,9 +55,9 @@ def tile_attend_plw_cfg_topk_kernel(tc, qT, k_words, k_scales, c_words, c_scales
 
         nc.sync.dma_start(q_raw[:], qT[0].rearrange("(p j) w -> p j w", j=PACK))
         nc.sync.dma_start(offsets[:], offs)
-        nc.sync.dma_start(ls_rows[0:QT, :], ls[0, 0].rearrange("(t p) -> t p", p=P))
         for j in range(ROWS):
             nc.sync.dma_start(ks_pool[j:P:QUAD, :].bitcast(I32), k_scales[0, j:ROWS * ROWS:ROWS, :].bitcast(I32))
+        nc.sync.dma_start(ls_rows[0:QT, :], ls[0, 0].rearrange("(t p) -> t p", p=P))
         nc.sync.dma_start(k_pool[:].bitcast(I32), as_words(k_words))
         for j in range(ROWS):
             nc.sync.dma_start(cs_pool[C_ROW + j:P:QUAD, :].bitcast(I32), c_scales[0, j:ROWS * ROWS:ROWS, :].bitcast(I32))
@@ -69,8 +69,8 @@ def tile_attend_plw_cfg_topk_kernel(tc, qT, k_words, k_scales, c_words, c_scales
         nc.scalar.activation(neg_ls[:], ls_ps[:, 0:QT], ACT.Copy, scale=-1.0)
 
         ksg = keep.tile([P, SLOTS], U8, name="ksg", align_bytes=64)
-        kg = [keep.tile([P, HALF], U32, name="kg%d" % h, align_bytes=64) for h in range(2)]
-        cg = [keep.tile([P, HALF], U32, name="cg%d" % h, align_bytes=64) for h in range(2)]
+        kg = keep.tile([P, SLOTS], U32, name="kg", align_bytes=64)
+        cg = keep.tile([P, SLOTS], U32, name="cg", align_bytes=64)
         nc.vector.tensor_copy(ksg[:], ks_pool[:].indirect(offsets[:]))
 
         q_bf = []
@@ -94,38 +94,35 @@ def tile_attend_plw_cfg_topk_kernel(tc, qT, k_words, k_scales, c_words, c_scales
             q_scales.append(scales)
 
         def gather_words(dst, pool, h):
-            nc.vector.tensor_copy(dst[h][:], pool[:].indirect(offsets[:, h * (HALF // 16):(h + 1) * (HALF // 16)]))
+            nc.vector.tensor_copy(dst[:, h * HALF:(h + 1) * HALF], pool[:].indirect(offsets[:, h * (HALF // 16):(h + 1) * (HALF // 16)]))
 
         quantise_q(0)
         quantise_q(1)
         gather_words(kg, k_pool, 0)
         gather_words(kg, k_pool, 1)
-        csg = keep.tile([P, SLOTS], U8, name="csg", tag="k_pool", align_bytes=64)
+        csg = keep.tile([P, SLOTS], U8, name="csg", align_bytes=64)
         nc.vector.tensor_copy(csg[:], cs_pool[:].indirect(offsets[:]))
 
         def scores(out, t, h, words, scales, first_row):
             cols = slice((t % 2) * P, (t % 2 + 1) * P)
-            slots = slice(h * HALF, (h + 1) * HALF)
+            slots = slice(0, SLOTS) if h is None else slice(h * HALF, (h + 1) * HALF)
             nc.tensor.matmul_mx(out=out, lhsT=q_codes[t // 2][:, cols].bitcast(FP8X4), lhsT_scale=q_scales[t // 2][:, cols],
-                                rhs=words[h][:].bitcast(FP8X4), rhs_scale=scales[first_row:P, slots], start=True, stop=True)
+                                rhs=words[:, slots].bitcast(FP8X4), rhs_scale=scales[first_row:P, slots], start=True, stop=True)
 
         def dealt(bank):
             return bank.rearrange("p (s r) -> p r s", r=PACK)
 
-        warm = psum.tile([P, HALF], F32, name="warm", tag="bank%d" % (2 * QT - 2))
-        for repeat in range(3):
-            nc.tensor.matmul_mx(out=warm[:], lhsT=q_codes[1][:, 0:P].bitcast(FP8X4), lhsT_scale=q_scales[1][:, 0:P],
-                                rhs=q_codes[1].bitcast(FP8X4), rhs_scale=q_scales[1][:], start=True, stop=True)
-
         a = [psum.tile([P, SLOTS], F32, name="a_ps%d" % t, tag="bank%d" % t) for t in range(QT)]
         u = [keep.tile([P, PACK, 2, P], F32, name="u%d" % g) for g in range(2)]
         w = [keep.tile([P, PACK, 2, P], F32, name="w%d" % g) for g in range(2)]
-        for g in range(2):
-            for h in range(2):
-                for t in range(2 * g, 2 * g + 2):
-                    scores(a[t][:, h * HALF:(h + 1) * HALF], t, h, kg, ksg, 0)
-            for t in range(2 * g, 2 * g + 2):
-                nc.scalar.activation(u[g][:, :, t % 2, :], dealt(a[t][:]), ACT.Identity, bias=neg_ls[:, t:t + 1], scale=1.5)
+        for t in range(2):
+            scores(a[t][:, 0:HALF], t, 0, kg, ksg, 0)
+        for t in range(QT):
+            if t < 2:
+                scores(a[t][:, HALF:SLOTS], t, 1, kg, ksg, 0)
+            else:
+                scores(a[t][:], t, None, kg, ksg, 0)
+            nc.scalar.activation(u[t // 2][:, :, t % 2, :], dealt(a[t][:]), ACT.Identity, bias=neg_ls[:, t:t + 1], scale=1.5)
         gather_words(cg, c_pool, 0)
         gather_words(cg, c_pool, 1)
 
@@ -143,36 +140,48 @@ def tile_attend_plw_cfg_topk_kernel(tc, qT, k_words, k_scales, c_words, c_scales
             for t in range(2):
                 scores(z_half[h][:, t, :], t, h, cg, csg, C_ROW)
         for t in range(2):
-            for h in range(2):
-                scores(z_tile[t][:, h * HALF:(h + 1) * HALF], 2 + t, h, cg, csg, C_ROW)
+            scores(z_tile[t][:], 2 + t, None, cg, csg, C_ROW)
 
         def exponent(out, z, u_part):
             nc.vector.scalar_tensor_tensor(out, dealt(z), -0.5, u_part, ALU.mult, ALU.add)
 
         exponent(half_of(w[0], 0), z_half[0][:].rearrange("p t n -> p (t n)"), half_of(u[0], 0))
-        for t in range(2):
-            exponent(w[0][:, :, t, P // 2:P], z_half[1][:, t, :], u[0][:, :, t, P // 2:P])
+        for places in (slice(0, 2), slice(2, PACK)):
+            nc.vector.scalar_tensor_tensor(w[0][:, places, 0, P // 2:P], dealt(z_half[1][:, 0, :])[:, places, :], -0.5,
+                                           u[0][:, places, 0, P // 2:P], ALU.mult, ALU.add)
+        exponent(w[0][:, :, 1, P // 2:P], z_half[1][:, 1, :], u[0][:, :, 1, P // 2:P])
         for t in range(2):
             exponent(w[1][:, :, t, :], z_tile[t][:], u[1][:, :, t, :])
 
         y = [keep.tile([P, PACK, P], F32, name="y%d" % t) for t in range(QT)]
         y_bf = keep.tile([P, NQ, PACK], BF16, name="y_bf", align_bytes=64)
         for t in range(QT):
-            turned = psum.tile([P, PACK, P], F32, name="turned%d" % t, tag="bank%d" % t)
-            for r in range(PACK):
-                nc.tensor.transpose(turned[:, r, :], w[t // 2][:, r, t % 2, :], ident[:])
-            if t == QT - 1:
-                nc.scalar.activation(y_bf[:, t * P:(t + 1) * P, :], turned[:].rearrange("p r q -> p q r"), ACT.Exp)
-            nc.scalar.activation(y[t][:], turned[:], ACT.Exp)
+            banks = (0, QT) if t == 0 else (t,)
+            count = PACK // len(banks)
+            for part, bank in enumerate(banks):
+                turned = psum.tile([P, count, P], F32, name="turned%d_%d" % (t, part), tag="bank%d" % bank)
+                for r in range(count):
+                    nc.tensor.transpose(turned[:, r, :], w[t // 2][:, part * count + r, t % 2, :], ident[:])
+                nc.scalar.activation(y[t][:, part * count:(part + 1) * count, :], turned[:], ACT.Exp)
             nc.sync.dma_start(y_rows[:, :, t * P:(t + 1) * P], y[t][:])
+        nc.scalar.activation(y_bf[:, NQ - P:NQ, :], turned[:].rearrange("p r q -> p q r"), ACT.Exp)
 
-        for g in range(2):
-            for t in range(2 * g, min(2 * g + 2, QT - 1)):
-                nc.vector.tensor_copy(*woven(y_bf[:, t * P:(t + 1) * P, :], y[t][:]))
-            cols = slice(g * HALF, (g + 1) * HALF)
+        def round_y(t):
+            nc.vector.tensor_copy(*woven(y_bf[:, t * P:(t + 1) * P, :], y[t][:]))
+
+        def quantise_y(t):
+            cols = slice(t * P, (t + 1) * P)
             nc.vector.quantize_mx(out=y_codes[:, cols].bitcast(FP8X4), scales=y_scales[:, cols],
                                   in_=y_bf[:, cols, :].rearrange("p w j -> p (w j)"))
-            nc.sync.dma_start(y_words[:, cols], y_codes[:, cols].bitcast(I32))
+            if t % 2 == 1:
+                pair = slice((t - 1) * P, (t + 1) * P)
+                nc.sync.dma_start(y_words[:, pair], y_codes[:, pair].bitcast(I32))
+
+        round_y(0)
+        for t in range(QT):
+            if t + 1 < QT - 1:
+                round_y(t + 1)
+            quantise_y(t)
         for j in range(ROWS):
             queue = nc.sync if j == 0 else nc.scalar
             queue.dma_start(out_2[0, j:ROWS * ROWS:ROWS, :].bitcast(I32), y_scales[j:P:QUAD, :].bitcast(I32))

@@ -146,28 +146,35 @@ def tile_attend_plw_cfg_topk_kernel(tc, qT, k_words, k_scales, c_words, c_scales
             nc.vector.scalar_tensor_tensor(out, dealt(z), -0.5, u_part, ALU.mult, ALU.add)
 
         exponent(half_of(w[0], 0), z_half[0][:].rearrange("p t n -> p (t n)"), half_of(u[0], 0))
-        for places in (slice(0, 2), slice(2, PACK)):
-            nc.vector.scalar_tensor_tensor(w[0][:, places, 0, P // 2:P], dealt(z_half[1][:, 0, :])[:, places, :], -0.5,
-                                           u[0][:, places, 0, P // 2:P], ALU.mult, ALU.add)
-        exponent(w[0][:, :, 1, P // 2:P], z_half[1][:, 1, :], u[0][:, :, 1, P // 2:P])
+        for first in (0, 2):
+            nc.vector.scalar_tensor_tensor(half_of(w[0], 1)[:, 2 * first:2 * first + 4, :],
+                                           dealt(z_half[1][:].rearrange("p t n -> p (t n)"))[:, first:first + 2, :], -0.5,
+                                           half_of(u[0], 1)[:, 2 * first:2 * first + 4, :], ALU.mult, ALU.add)
         for t in range(2):
             exponent(w[1][:, :, t, :], z_tile[t][:], u[1][:, :, t, :])
 
-        y = [keep.tile([P, PACK, P], F32, name="y%d" % t) for t in range(QT)]
+        y = keep.tile([P, PACK, NQ], F32, name="y")
         y_bf = keep.tile([P, NQ, PACK], BF16, name="y_bf", align_bytes=64)
-        for t in range(QT):
-            banks = (0, QT) if t == 0 else (t,)
-            count = PACK // len(banks)
-            for part, bank in enumerate(banks):
-                turned = psum.tile([P, count, P], F32, name="turned%d_%d" % (t, part), tag="bank%d" % bank)
-                for r in range(count):
-                    nc.tensor.transpose(turned[:, r, :], w[t // 2][:, part * count + r, t % 2, :], ident[:])
-                nc.scalar.activation(y[t][:, part * count:(part + 1) * count, :], turned[:], ACT.Exp)
-            nc.sync.dma_start(y_rows[:, :, t * P:(t + 1) * P], y[t][:])
-        nc.scalar.activation(y_bf[:, NQ - P:NQ, :], turned[:].rearrange("p r q -> p q r"), ACT.Exp)
+
+        def finish(bank, places, tiles):
+            turned = psum.tile([P, len(places), len(tiles), P], F32, name="turned%d" % bank, tag="bank%d" % bank)
+            for r in places:
+                for t in tiles:
+                    nc.tensor.transpose(turned[:, r - places.start, t - tiles.start, :], w[t // 2][:, r, t % 2, :], ident[:])
+            rows, cols = slice(places.start, places.stop), slice(tiles.start * P, tiles.stop * P)
+            nc.scalar.activation(y[:, rows, cols], turned[:].rearrange("p r t q -> p r (t q)"), ACT.Exp)
+            nc.sync.dma_start(y_rows[:, rows, cols], y[:, rows, cols])
+            return turned
+
+        finish(0, range(0, 1), range(0, 2))
+        finish(QT, range(1, 2), range(0, 2))
+        finish(1, range(2, PACK), range(0, 2))
+        finish(2, range(0, PACK), range(2, 3))
+        last = finish(3, range(0, PACK), range(3, QT))
+        nc.scalar.activation(y_bf[:, NQ - P:NQ, :], last[:].rearrange("p r t q -> p (t q) r"), ACT.Exp)
 
         def round_y(t):
-            nc.vector.tensor_copy(*woven(y_bf[:, t * P:(t + 1) * P, :], y[t][:]))
+            nc.vector.tensor_copy(*woven(y_bf[:, t * P:(t + 1) * P, :], y[:, :, t * P:(t + 1) * P]))
 
         def quantise_y(t):
             cols = slice(t * P, (t + 1) * P)

@@ -146,10 +146,10 @@ def tile_attend_plw_cfg_topk_kernel(tc, qT, k_words, k_scales, c_words, c_scales
             nc.vector.scalar_tensor_tensor(out, dealt(z), -0.5, u_part, ALU.mult, ALU.add)
 
         exponent(half_of(w[0], 0), z_half[0][:].rearrange("p t n -> p (t n)"), half_of(u[0], 0))
-        for first in (0, 2):
-            nc.vector.scalar_tensor_tensor(half_of(w[0], 1)[:, 2 * first:2 * first + 4, :],
-                                           dealt(z_half[1][:].rearrange("p t n -> p (t n)"))[:, first:first + 2, :], -0.5,
-                                           half_of(u[0], 1)[:, 2 * first:2 * first + 4, :], ALU.mult, ALU.add)
+        for first, stop in ((0, 1), (1, 2), (2, PACK)):
+            nc.vector.scalar_tensor_tensor(half_of(w[0], 1)[:, 2 * first:2 * stop, :],
+                                           dealt(z_half[1][:].rearrange("p t n -> p (t n)"))[:, first:stop, :], -0.5,
+                                           half_of(u[0], 1)[:, 2 * first:2 * stop, :], ALU.mult, ALU.add)
         for t in range(2):
             exponent(w[1][:, :, t, :], z_tile[t][:], u[1][:, :, t, :])
 
@@ -169,9 +169,15 @@ def tile_attend_plw_cfg_topk_kernel(tc, qT, k_words, k_scales, c_words, c_scales
         finish(0, range(0, 1), range(0, 2))
         finish(QT, range(1, 2), range(0, 2))
         finish(1, range(2, PACK), range(0, 2))
-        finish(2, range(0, PACK), range(2, 3))
-        last = finish(3, range(0, PACK), range(3, QT))
-        nc.scalar.activation(y_bf[:, NQ - P:NQ, :], last[:].rearrange("p r t q -> p (t q) r"), ACT.Exp)
+        turned = [psum.tile([P, PACK, P], F32, name="turned_tile%d" % t, tag="bank%d" % (2 + t)) for t in range(2)]
+        for t in range(2):
+            for r in range(PACK):
+                nc.tensor.transpose(turned[t][:, r, :], w[1][:, r, t, :], ident[:])
+        for first in (0, 2):
+            for t in range(2):
+                nc.scalar.activation(y[:, first:first + 2, HALF + t * P:HALF + (t + 1) * P], turned[t][:, first:first + 2, :], ACT.Exp)
+            nc.sync.dma_start(y_rows[:, first:first + 2, HALF:NQ], y[:, first:first + 2, HALF:NQ])
+        nc.scalar.activation(y_bf[:, NQ - P:NQ, :], turned[1][:].rearrange("p r q -> p q r"), ACT.Exp)
 
         def round_y(t):
             nc.vector.tensor_copy(*woven(y_bf[:, t * P:(t + 1) * P, :], y[:, :, t * P:(t + 1) * P]))

@@ -186,15 +186,13 @@ def tile_attend_plw_cfg_topk_kernel(tc, qT, k_words, k_scales, c_words, c_scales
             cols = slice(t * P, (t + 1) * P)
             nc.vector.quantize_mx(out=y_codes[:, cols].bitcast(FP8X4), scales=y_scales[:, cols],
                                   in_=y_bf[:, cols, :].rearrange("p w j -> p (w j)"))
-            if t % 2 == 1:
-                pair = slice((t - 1) * P, (t + 1) * P)
-                nc.sync.dma_start(y_words[:, pair], y_codes[:, pair].bitcast(I32))
 
         round_y(0)
         for t in range(QT):
             if t + 1 < QT - 1:
                 round_y(t + 1)
             quantise_y(t)
+        nc.sync.dma_start(y_words, y_codes[:].bitcast(I32))
         for j in range(ROWS):
             queue = nc.sync if j == 0 else nc.scalar
             queue.dma_start(out_2[0, j:ROWS * ROWS:ROWS, :].bitcast(I32), y_scales[j:P:QUAD, :].bitcast(I32))

@@ -20,7 +20,8 @@ ROWS = 4
 SLOTS, TOKENS, D, NQ = 512, 2048, 512, 512
 QT = NQ // P
 HALF = NQ // 2
-C_ROW = 4
+BLOCKS = D // 32
+K_ROW, C_ROW = 112, 48
 LINE = 4
 
 FLOPS = 2 * 2 * SLOTS * D * NQ
@@ -46,32 +47,46 @@ def tile_attend_plw_cfg_topk_kernel(tc, qT, k_words, k_scales, c_words, c_scales
         ident = keep.tile([P, P], F32, name="ident")
         q_raw = keep.tile([P, PACK, NQ], F32, name="q_raw")
         k_pool = keep.tile([P, TOKENS], U32, name="k_pool", align_bytes=64)
-        c_pool = keep.tile([P, TOKENS], U32, name="c_pool", align_bytes=64)
+        planes = keep.tile([P, 2, SLOTS], U8, name="planes", align_bytes=64)
 
-        nc.gpsimd.memset(ls_rows[:], 0.0)
-        nc.vector.memset(ks_pool[:].bitcast(I32), 0)
-        nc.vector.memset(cs_pool[:].bitcast(I32), 0)
-        make_identity(nc, ident[:])
+        zero = keep.tile([P, 1], F32, name="zero")
+        nc.vector.memset(ks_pool[0:K_ROW, :].bitcast(I32), 0)
+        nc.vector.memset(zero[:], 0.0)
+        nc.vector.memset(cs_pool[0:C_ROW, :].bitcast(I32), 0)
+        nc.vector.memset(cs_pool[C_ROW + BLOCKS:P, :].bitcast(I32), 0)
+        nc.vector.memset(ident[:], 0.0)
+        nc.scalar.activation(ls_rows[0:P - QT, :], zero[0:P - QT, :].to_broadcast([P - QT, P]), ACT.Copy)
+        nc.vector.memset(planes[:].rearrange("p t n -> p (t n)").bitcast(I32), 0)
+        make_identity(nc, ident[:], nomemset=True)
 
-        nc.sync.dma_start(q_raw[:], qT[0].rearrange("(p j) w -> p j w", j=PACK))
+        q_rows = qT[0].rearrange("(p j) w -> p j w", j=PACK)
+        nc.sync.dma_start(q_raw[:, 0:1, :], q_rows[:, 0:1, :])
         nc.sync.dma_start(offsets[:], offs)
-        for j in range(ROWS):
-            nc.sync.dma_start(ks_pool[j:P:QUAD, :].bitcast(I32), k_scales[0, j:ROWS * ROWS:ROWS, :].bitcast(I32))
-        nc.sync.dma_start(ls_rows[0:QT, :], ls[0, 0].rearrange("(t p) -> t p", p=P))
+        nc.sync.dma_start(ks_pool[K_ROW:K_ROW + BLOCKS, :].bitcast(I32), k_scales[0].bitcast(I32))
+        nc.sync.dma_start(cs_pool[C_ROW:C_ROW + BLOCKS, :].bitcast(I32), c_scales[0].bitcast(I32))
+        nc.sync.dma_start(q_raw[:, 1:PACK, :], q_rows[:, 1:PACK, :])
+        nc.sync.dma_start(ls_rows[P - QT:P, :], ls[0, 0].rearrange("(t p) -> t p", p=P))
         nc.sync.dma_start(k_pool[:].bitcast(I32), as_words(k_words))
-        for j in range(ROWS):
-            nc.sync.dma_start(cs_pool[C_ROW + j:P:QUAD, :].bitcast(I32), c_scales[0, j:ROWS * ROWS:ROWS, :].bitcast(I32))
-        nc.sync.dma_start(c_pool[:].bitcast(I32), as_words(c_words))
+
+        def to_plane(table, gathered, first_row):
+            for j in range(ROWS):
+                nc.sync.dma_start(planes[j:P:QUAD, table, :].bitcast(I32), gathered[first_row + j:first_row + BLOCKS:ROWS, :].bitcast(I32))
 
         ls_ps = psum.tile([P, P], F32, name="ls_ps", tag="bank%d" % (2 * QT - 1))
         nc.tensor.transpose(ls_ps[:], ls_rows[:], ident[:])
         neg_ls = keep.tile([P, QT], F32, name="neg_ls")
-        nc.scalar.activation(neg_ls[:], ls_ps[:, 0:QT], ACT.Copy, scale=-1.0)
+        nc.scalar.activation(neg_ls[:], ls_ps[:, P - QT:P], ACT.Copy, scale=-1.0)
 
         ksg = keep.tile([P, SLOTS], U8, name="ksg", align_bytes=64)
         kg = keep.tile([P, SLOTS], U32, name="kg", align_bytes=64)
         cg = keep.tile([P, SLOTS], U32, name="cg", align_bytes=64)
+        csg = keep.tile([P, SLOTS], U8, name="csg", align_bytes=64)
         nc.vector.tensor_copy(ksg[:], ks_pool[:].indirect(offsets[:]))
+        to_plane(0, ksg, K_ROW)
+        c_pool = keep.tile([P, TOKENS], U32, name="c_pool", tag="ks_pool", align_bytes=64)
+        nc.sync.dma_start(c_pool[:].bitcast(I32), as_words(c_words))
+        nc.vector.tensor_copy(csg[:], cs_pool[:].indirect(offsets[:]))
+        to_plane(1, csg, C_ROW)
 
         q_bf = []
         for h in range(2):
@@ -84,7 +99,7 @@ def tile_attend_plw_cfg_topk_kernel(tc, qT, k_words, k_scales, c_words, c_scales
             q_bf.append(rounded)
 
         q_codes, q_scales = [], []
-        all_codes = keep.tile([P, NQ], U32, name="q_codes", tag="ks_pool", align_bytes=64)
+        all_codes = keep.tile([P, NQ], U32, name="q_codes", tag="cs_pool", align_bytes=64)
 
         def quantise_q(h):
             codes = all_codes[:, h * HALF:(h + 1) * HALF]
@@ -100,14 +115,12 @@ def tile_attend_plw_cfg_topk_kernel(tc, qT, k_words, k_scales, c_words, c_scales
         quantise_q(1)
         gather_words(kg, k_pool, 0)
         gather_words(kg, k_pool, 1)
-        csg = keep.tile([P, SLOTS], U8, name="csg", align_bytes=64)
-        nc.vector.tensor_copy(csg[:], cs_pool[:].indirect(offsets[:]))
 
-        def scores(out, t, h, words, scales, first_row):
+        def scores(out, t, h, words, table):
             cols = slice((t % 2) * P, (t % 2 + 1) * P)
             slots = slice(0, SLOTS) if h is None else slice(h * HALF, (h + 1) * HALF)
             nc.tensor.matmul_mx(out=out, lhsT=q_codes[t // 2][:, cols].bitcast(FP8X4), lhsT_scale=q_scales[t // 2][:, cols],
-                                rhs=words[:, slots].bitcast(FP8X4), rhs_scale=scales[first_row:P, slots], start=True, stop=True)
+                                rhs=words[:, slots].bitcast(FP8X4), rhs_scale=planes[:, table, slots], start=True, stop=True)
 
         def dealt(bank):
             return bank.rearrange("p (s r) -> p r s", r=PACK)
@@ -116,12 +129,12 @@ def tile_attend_plw_cfg_topk_kernel(tc, qT, k_words, k_scales, c_words, c_scales
         u = [keep.tile([P, PACK, 2, P], F32, name="u%d" % g) for g in range(2)]
         w = [keep.tile([P, PACK, 2, P], F32, name="w%d" % g) for g in range(2)]
         for t in range(2):
-            scores(a[t][:, 0:HALF], t, 0, kg, ksg, 0)
+            scores(a[t][:, 0:HALF], t, 0, kg, 0)
         for t in range(QT):
             if t < 2:
-                scores(a[t][:, HALF:SLOTS], t, 1, kg, ksg, 0)
+                scores(a[t][:, HALF:SLOTS], t, 1, kg, 0)
             else:
-                scores(a[t][:], t, None, kg, ksg, 0)
+                scores(a[t][:], t, None, kg, 0)
             nc.scalar.activation(u[t // 2][:, :, t % 2, :], dealt(a[t][:]), ACT.Identity, bias=neg_ls[:, t:t + 1], scale=1.5)
         gather_words(cg, c_pool, 0)
         gather_words(cg, c_pool, 1)
@@ -138,9 +151,9 @@ def tile_attend_plw_cfg_topk_kernel(tc, qT, k_words, k_scales, c_words, c_scales
         z_tile = [psum.tile([P, SLOTS], F32, name="z_tile%d" % t, tag="bank%d" % (QT + 2 + t)) for t in range(2)]
         for h in range(2):
             for t in range(2):
-                scores(z_half[h][:, t, :], t, h, cg, csg, C_ROW)
+                scores(z_half[h][:, t, :], t, h, cg, 1)
         for t in range(2):
-            scores(z_tile[t][:], 2 + t, None, cg, csg, C_ROW)
+            scores(z_tile[t][:], 2 + t, None, cg, 1)
 
         def exponent(out, z, u_part):
             nc.vector.scalar_tensor_tensor(out, dealt(z), -0.5, u_part, ALU.mult, ALU.add)
@@ -163,12 +176,12 @@ def tile_attend_plw_cfg_topk_kernel(tc, qT, k_words, k_scales, c_words, c_scales
                     nc.tensor.transpose(turned[:, r - places.start, t - tiles.start, :], w[t // 2][:, r, t % 2, :], ident[:])
             rows, cols = slice(places.start, places.stop), slice(tiles.start * P, tiles.stop * P)
             nc.scalar.activation(y[:, rows, cols], turned[:].rearrange("p r t q -> p r (t q)"), ACT.Exp)
-            nc.sync.dma_start(y_rows[:, rows, cols], y[:, rows, cols])
-            return turned
 
         finish(0, range(0, 1), range(0, 2))
         finish(QT, range(1, 2), range(0, 2))
+        nc.sync.dma_start(y_rows[:, 0:2, 0:HALF], y[:, 0:2, 0:HALF])
         finish(1, range(2, PACK), range(0, 2))
+        nc.sync.dma_start(y_rows[:, 2:PACK, 0:HALF], y[:, 2:PACK, 0:HALF])
         turned = [psum.tile([P, PACK, P], F32, name="turned_tile%d" % t, tag="bank%d" % (2 + t)) for t in range(2)]
         for t in range(2):
             for r in range(PACK):
@@ -192,7 +205,9 @@ def tile_attend_plw_cfg_topk_kernel(tc, qT, k_words, k_scales, c_words, c_scales
             if t + 1 < QT - 1:
                 round_y(t + 1)
             quantise_y(t)
-        nc.sync.dma_start(y_words, y_codes[:].bitcast(I32))
+            if t % 2 == 1:
+                cols = slice((t - 1) * P, (t + 1) * P)
+                nc.sync.dma_start(y_words[:, cols], y_codes[:, cols].bitcast(I32))
         for j in range(ROWS):
             queue = nc.sync if j == 0 else nc.scalar
             queue.dma_start(out_2[0, j:ROWS * ROWS:ROWS, :].bitcast(I32), y_scales[j:P:QUAD, :].bitcast(I32))

@@ -101,25 +101,28 @@ def tile_attend_plw_cfg_topk_kernel(tc, qT, k_words, k_scales, c_words, c_scales
         q_codes, q_scales = [], []
         all_codes = keep.tile([P, NQ], U32, name="q_codes", tag="cs_pool", align_bytes=64)
 
-        def quantise_q(h):
-            codes = all_codes[:, h * HALF:(h + 1) * HALF]
-            scales = keep.tile([P, HALF], U8, name="q_scales%d" % h, align_bytes=64)
-            nc.vector.quantize_mx(out=codes.bitcast(FP8X4), scales=scales[:], in_=q_bf[h][:].rearrange("p w j -> p (w j)"))
-            q_codes.append(codes)
-            q_scales.append(scales)
+        def quantise_q(tiles, tag):
+            first, width = tiles.start * P, len(tiles) * P
+            scales = keep.tile([P, width], U8, name="q_scales%d" % tiles.start, tag=tag, align_bytes=64)
+            rounded = q_bf[first // HALF][:, first % HALF:first % HALF + width, :]
+            nc.vector.quantize_mx(out=all_codes[:, first:first + width].bitcast(FP8X4), scales=scales[:],
+                                  in_=rounded.rearrange("p w j -> p (w j)"))
+            for t in tiles:
+                q_codes.append(all_codes[:, t * P:(t + 1) * P])
+                q_scales.append(scales[:, t * P - first:(t + 1) * P - first])
 
         def gather_words(dst, pool, h):
             nc.vector.tensor_copy(dst[:, h * HALF:(h + 1) * HALF], pool[:].indirect(offsets[:, h * (HALF // 16):(h + 1) * (HALF // 16)]))
 
-        quantise_q(0)
-        quantise_q(1)
+        quantise_q(range(0, 2), "q_scales0")
+        quantise_q(range(2, 3), "q_scales2")
         gather_words(kg, k_pool, 0)
         gather_words(kg, k_pool, 1)
+        quantise_q(range(QT - 1, QT), "k_pool")
 
         def scores(out, t, h, words, table):
-            cols = slice((t % 2) * P, (t % 2 + 1) * P)
             slots = slice(0, SLOTS) if h is None else slice(h * HALF, (h + 1) * HALF)
-            nc.tensor.matmul_mx(out=out, lhsT=q_codes[t // 2][:, cols].bitcast(FP8X4), lhsT_scale=q_scales[t // 2][:, cols],
+            nc.tensor.matmul_mx(out=out, lhsT=q_codes[t].bitcast(FP8X4), lhsT_scale=q_scales[t],
                                 rhs=words[:, slots].bitcast(FP8X4), rhs_scale=planes[:, table, slots], start=True, stop=True)
 
         def dealt(bank):
@@ -130,12 +133,15 @@ def tile_attend_plw_cfg_topk_kernel(tc, qT, k_words, k_scales, c_words, c_scales
         w = [keep.tile([P, PACK, 2, P], F32, name="w%d" % g) for g in range(2)]
         for t in range(2):
             scores(a[t][:, 0:HALF], t, 0, kg, 0)
-        for t in range(QT):
+        def first_term(t):
             if t < 2:
                 scores(a[t][:, HALF:SLOTS], t, 1, kg, 0)
             else:
                 scores(a[t][:], t, None, kg, 0)
             nc.scalar.activation(u[t // 2][:, :, t % 2, :], dealt(a[t][:]), ACT.Identity, bias=neg_ls[:, t:t + 1], scale=1.5)
+
+        for t in range(QT - 1):
+            first_term(t)
         gather_words(cg, c_pool, 0)
         gather_words(cg, c_pool, 1)
 
@@ -152,6 +158,8 @@ def tile_attend_plw_cfg_topk_kernel(tc, qT, k_words, k_scales, c_words, c_scales
         for h in range(2):
             for t in range(2):
                 scores(z_half[h][:, t, :], t, h, cg, 1)
+            if h == 0:
+                first_term(QT - 1)
         for t in range(2):
             scores(z_tile[t][:], 2 + t, None, cg, 1)
 

@@ -19,9 +19,9 @@ QUAD = 32
 ROWS = 4
 SLOTS, TOKENS, D, NQ = 512, 2048, 512, 512
 QT = NQ // P
-HALF = NQ // 2
+HALF = 256
 BLOCKS = D // 32
-K_ROW, C_ROW = 112, 48
+LOADED = P - BLOCKS
 LINE = 4
 
 FLOPS = 2 * 2 * SLOTS * D * NQ
@@ -49,28 +49,23 @@ def tile_attend_plw_cfg_topk_kernel(tc, qT, k_words, k_scales, c_words, c_scales
         k_pool = keep.tile([P, TOKENS], U32, name="k_pool", align_bytes=64)
         planes = keep.tile([P, 2, SLOTS], U8, name="planes", align_bytes=64)
 
-        zero = keep.tile([P, 1], F32, name="zero")
-        nc.vector.memset(ks_pool[0:K_ROW, :].bitcast(I32), 0)
-        nc.vector.memset(zero[:], 0.0)
-        nc.vector.memset(cs_pool[0:C_ROW, :].bitcast(I32), 0)
-        nc.vector.memset(cs_pool[C_ROW + BLOCKS:P, :].bitcast(I32), 0)
+        nc.vector.memset(ks_pool[0:LOADED, :].bitcast(I32), 0)
+        nc.vector.memset(cs_pool[0:LOADED, :].bitcast(I32), 0)
         nc.vector.memset(ident[:], 0.0)
-        nc.scalar.activation(ls_rows[0:P - QT, :], zero[0:P - QT, :].to_broadcast([P - QT, P]), ACT.Copy)
+        nc.vector.memset(ls_rows[0:P - QT, :], 0.0)
         nc.vector.memset(planes[:].rearrange("p t n -> p (t n)").bitcast(I32), 0)
         make_identity(nc, ident[:], nomemset=True)
 
-        q_rows = qT[0].rearrange("(p j) w -> p j w", j=PACK)
-        nc.sync.dma_start(q_raw[:, 0:1, :], q_rows[:, 0:1, :])
         nc.sync.dma_start(offsets[:], offs)
-        nc.sync.dma_start(ks_pool[K_ROW:K_ROW + BLOCKS, :].bitcast(I32), k_scales[0].bitcast(I32))
-        nc.sync.dma_start(cs_pool[C_ROW:C_ROW + BLOCKS, :].bitcast(I32), c_scales[0].bitcast(I32))
-        nc.sync.dma_start(q_raw[:, 1:PACK, :], q_rows[:, 1:PACK, :])
+        nc.sync.dma_start(ks_pool[LOADED:P, :].bitcast(I32), k_scales[0].bitcast(I32))
+        nc.sync.dma_start(q_raw[:], qT[0].rearrange("(p j) w -> p j w", j=PACK))
+        nc.sync.dma_start(cs_pool[LOADED:P, :].bitcast(I32), c_scales[0].bitcast(I32))
         nc.sync.dma_start(ls_rows[P - QT:P, :], ls[0, 0].rearrange("(t p) -> t p", p=P))
         nc.sync.dma_start(k_pool[:].bitcast(I32), as_words(k_words))
 
-        def to_plane(table, gathered, first_row):
+        def to_plane(table, gathered):
             for j in range(ROWS):
-                nc.sync.dma_start(planes[j:P:QUAD, table, :].bitcast(I32), gathered[first_row + j:first_row + BLOCKS:ROWS, :].bitcast(I32))
+                nc.sync.dma_start(planes[j:P:QUAD, table, :].bitcast(I32), gathered[LOADED + j:P:ROWS, :].bitcast(I32))
 
         ls_ps = psum.tile([P, P], F32, name="ls_ps", tag="bank%d" % (2 * QT - 1))
         nc.tensor.transpose(ls_ps[:], ls_rows[:], ident[:])
@@ -82,11 +77,11 @@ def tile_attend_plw_cfg_topk_kernel(tc, qT, k_words, k_scales, c_words, c_scales
         cg = keep.tile([P, SLOTS], U32, name="cg", align_bytes=64)
         csg = keep.tile([P, SLOTS], U8, name="csg", align_bytes=64)
         nc.vector.tensor_copy(ksg[:], ks_pool[:].indirect(offsets[:]))
-        to_plane(0, ksg, K_ROW)
+        to_plane(0, ksg)
         c_pool = keep.tile([P, TOKENS], U32, name="c_pool", tag="ks_pool", align_bytes=64)
         nc.sync.dma_start(c_pool[:].bitcast(I32), as_words(c_words))
         nc.vector.tensor_copy(csg[:], cs_pool[:].indirect(offsets[:]))
-        to_plane(1, csg, C_ROW)
+        to_plane(1, csg)
 
         q_bf = []
         for h in range(2):
@@ -133,6 +128,7 @@ def tile_attend_plw_cfg_topk_kernel(tc, qT, k_words, k_scales, c_words, c_scales
         w = [keep.tile([P, PACK, 2, P], F32, name="w%d" % g) for g in range(2)]
         for t in range(2):
             scores(a[t][:, 0:HALF], t, 0, kg, 0)
+
         def first_term(t):
             if t < 2:
                 scores(a[t][:, HALF:SLOTS], t, 1, kg, 0)

@@ -57,7 +57,7 @@ def tile_attend_plw_cfg_topk_kernel(tc, qT, k_words, k_scales, c_words, c_scales
         make_identity(nc, ident[:], nomemset=True)
 
         nc.sync.dma_start(offsets[:], offs)
-        nc.sync.dma_start(ks_pool[LOADED:P, :].bitcast(I32), k_scales[0].bitcast(I32))
+        nc.scalar.dma_start(ks_pool[LOADED:P, :].bitcast(I32), k_scales[0].bitcast(I32))
         nc.sync.dma_start(q_raw[:], qT[0].rearrange("(p j) w -> p j w", j=PACK))
         nc.sync.dma_start(cs_pool[LOADED:P, :].bitcast(I32), c_scales[0].bitcast(I32))
         nc.sync.dma_start(ls_rows[P - QT:P, :], ls[0, 0].rearrange("(t p) -> t p", p=P))
@@ -209,9 +209,7 @@ def tile_attend_plw_cfg_topk_kernel(tc, qT, k_words, k_scales, c_words, c_scales
             if t + 1 < QT - 1:
                 round_y(t + 1)
             quantise_y(t)
-            if t % 2 == 1:
-                cols = slice((t - 1) * P, (t + 1) * P)
-                nc.sync.dma_start(y_words[:, cols], y_codes[:, cols].bitcast(I32))
+        nc.sync.dma_start(y_words, y_codes[:].bitcast(I32))
         for j in range(ROWS):
             queue = nc.sync if j == 0 else nc.scalar
             queue.dma_start(out_2[0, j:ROWS * ROWS:ROWS, :].bitcast(I32), y_scales[j:P:QUAD, :].bitcast(I32))

@@ -123,7 +123,7 @@ def tile_attend_plw_cfg_topk_kernel(tc, qT, k_words, k_scales, c_words, c_scales
         def dealt(bank):
             return bank.rearrange("p (s r) -> p r s", r=PACK)
 
-        a = [psum.tile([P, SLOTS], F32, name="a_ps%d" % t, tag="bank%d" % t) for t in range(QT)]
+        a = [psum.tile([P, SLOTS], F32, name="a_ps%d" % t, tag="bank%d" % t) for t in range(QT - 1)]
         u = [keep.tile([P, PACK, 2, P], F32, name="u%d" % g) for g in range(2)]
         w = [keep.tile([P, PACK, 2, P], F32, name="w%d" % g) for g in range(2)]
         for t in range(2):
@@ -149,26 +149,37 @@ def tile_attend_plw_cfg_topk_kernel(tc, qT, k_words, k_scales, c_words, c_scales
         def half_of(pair, h):
             return pair[:].rearrange("p r t (h s) -> p (r t) h s", h=2)[:, :, h, :]
 
-        z_half = [psum.tile([P, 2, HALF], F32, name="z_half%d" % h, tag="bank%d" % (QT + h)) for h in range(2)]
+        z_first = [psum.tile([P, HALF], F32, name="z_first%d" % t, tag="bank%d" % (0, QT)[t]) for t in range(2)]
+        z_second = psum.tile([P, 2, HALF], F32, name="z_second", tag="bank%d" % (QT + 1))
         z_tile = [psum.tile([P, SLOTS], F32, name="z_tile%d" % t, tag="bank%d" % (QT + 2 + t)) for t in range(2)]
-        for h in range(2):
-            for t in range(2):
-                scores(z_half[h][:, t, :], t, h, cg, 1)
-            if h == 0:
-                first_term(QT - 1)
+
+        def last_first_term(h, bank):
+            part = psum.tile([P, HALF], F32, name="a_last%d" % h, tag="bank%d" % bank)
+            scores(part[:], QT - 1, h, kg, 0)
+            nc.scalar.activation(u[1][:, :, 1, h * (P // 2):(h + 1) * (P // 2)], dealt(part[:]), ACT.Identity, bias=neg_ls[:, QT - 1:QT], scale=1.5)
+
+        last_first_term(0, QT - 1)
+        for t in range(2):
+            scores(z_first[t][:], t, 0, cg, 1)
+        for t in range(2):
+            scores(z_second[:, t, :], t, 1, cg, 1)
         for t in range(2):
             scores(z_tile[t][:], 2 + t, None, cg, 1)
 
         def exponent(out, z, u_part):
             nc.vector.scalar_tensor_tensor(out, dealt(z), -0.5, u_part, ALU.mult, ALU.add)
 
-        exponent(half_of(w[0], 0), z_half[0][:].rearrange("p t n -> p (t n)"), half_of(u[0], 0))
+        for t in range(2):
+            exponent(w[0][:, :, t, 0:P // 2], z_first[t][:], u[0][:, :, t, 0:P // 2])
+        last_first_term(1, 0)
         for first, stop in ((0, 1), (1, 2), (2, PACK)):
             nc.vector.scalar_tensor_tensor(half_of(w[0], 1)[:, 2 * first:2 * stop, :],
-                                           dealt(z_half[1][:].rearrange("p t n -> p (t n)"))[:, first:stop, :], -0.5,
+                                           dealt(z_second[:].rearrange("p t n -> p (t n)"))[:, first:stop, :], -0.5,
                                            half_of(u[0], 1)[:, 2 * first:2 * stop, :], ALU.mult, ALU.add)
-        for t in range(2):
-            exponent(w[1][:, :, t, :], z_tile[t][:], u[1][:, :, t, :])
+        exponent(w[1][:, :, 0, :], z_tile[0][:], u[1][:, :, 0, :])
+        for first in (0, 2):
+            nc.vector.scalar_tensor_tensor(w[1][:, first:first + 2, 1, :], dealt(z_tile[1][:])[:, first:first + 2, :], -0.5,
+                                           u[1][:, first:first + 2, 1, :], ALU.mult, ALU.add)
 
         y = keep.tile([P, PACK, NQ], F32, name="y")
         y_bf = keep.tile([P, NQ, PACK], BF16, name="y_bf", align_bytes=64)
@@ -181,12 +192,12 @@ def tile_attend_plw_cfg_topk_kernel(tc, qT, k_words, k_scales, c_words, c_scales
             rows, cols = slice(places.start, places.stop), slice(tiles.start * P, tiles.stop * P)
             nc.scalar.activation(y[:, rows, cols], turned[:].rearrange("p r t q -> p r (t q)"), ACT.Exp)
 
-        finish(0, range(0, 1), range(0, 2))
-        finish(QT, range(1, 2), range(0, 2))
+        finish(QT, range(0, 1), range(0, 2))
+        finish(QT - 1, range(1, 2), range(0, 2))
         nc.sync.dma_start(y_rows[:, 0:2, 0:HALF], y[:, 0:2, 0:HALF])
         finish(1, range(2, PACK), range(0, 2))
         nc.sync.dma_start(y_rows[:, 2:PACK, 0:HALF], y[:, 2:PACK, 0:HALF])
-        turned = [psum.tile([P, PACK, P], F32, name="turned_tile%d" % t, tag="bank%d" % (2 + t)) for t in range(2)]
+        turned = [psum.tile([P, PACK, P], F32, name="turned_tile%d" % t, tag="bank%d" % (2, QT + 1)[t]) for t in range(2)]
         for t in range(2):
             for r in range(PACK):
                 nc.tensor.transpose(turned[t][:, r, :], w[1][:, r, t, :], ident[:])

@@ -201,25 +201,24 @@ def tile_attend_plw_cfg_topk_kernel(tc, qT, k_words, k_scales, c_words, c_scales
         for t in range(2):
             for r in range(PACK):
                 nc.tensor.transpose(turned[t][:, r, :], w[1][:, r, t, :], ident[:])
+        nc.scalar.activation(y[:, :, HALF:HALF + P], turned[0][:], ACT.Exp)
         for first in (0, 2):
-            for t in range(2):
-                nc.scalar.activation(y[:, first:first + 2, HALF + t * P:HALF + (t + 1) * P], turned[t][:, first:first + 2, :], ACT.Exp)
+            nc.scalar.activation(y[:, first:first + 2, NQ - P:NQ], turned[1][:, first:first + 2, :], ACT.Exp)
             nc.sync.dma_start(y_rows[:, first:first + 2, HALF:NQ], y[:, first:first + 2, HALF:NQ])
         nc.scalar.activation(y_bf[:, NQ - P:NQ, :], turned[1][:].rearrange("p r q -> p q r"), ACT.Exp)
 
-        def round_y(t):
-            nc.vector.tensor_copy(*woven(y_bf[:, t * P:(t + 1) * P, :], y[:, :, t * P:(t + 1) * P]))
+        def round_y(first, stop):
+            nc.vector.tensor_copy(*woven(y_bf[:, first:stop, :], y[:, :, first:stop]))
 
-        def quantise_y(t):
-            cols = slice(t * P, (t + 1) * P)
-            nc.vector.quantize_mx(out=y_codes[:, cols].bitcast(FP8X4), scales=y_scales[:, cols],
-                                  in_=y_bf[:, cols, :].rearrange("p w j -> p (w j)"))
+        def quantise_y(first, stop):
+            nc.vector.quantize_mx(out=y_codes[:, first:stop].bitcast(FP8X4), scales=y_scales[:, first:stop],
+                                  in_=y_bf[:, first:stop, :].rearrange("p w j -> p (w j)"))
 
-        round_y(0)
-        for t in range(QT):
-            if t + 1 < QT - 1:
-                round_y(t + 1)
-            quantise_y(t)
+        round_y(0, HALF)
+        round_y(HALF, HALF + P)
+        quantise_y(0, HALF)
+        quantise_y(HALF, HALF + P)
+        quantise_y(NQ - P, NQ)
         nc.sync.dma_start(y_words, y_codes[:].bitcast(I32))
         for j in range(ROWS):
             queue = nc.sync if j == 0 else nc.scalar

@@ -40,34 +40,40 @@ def tile_attend_plw_cfg_topk_kernel(tc, qT, k_words, k_scales, c_words, c_scales
         keep = ctx.enter_context(tc.tile_pool(name="keep", bufs=1))
         psum = ctx.enter_context(tc.psum_pool(name="psum", bufs=1))
 
+        def bank(number, name, shape):
+            return psum.tile([P] + shape, F32, name=name, tag="bank%d" % number)
+
         offsets = keep.tile([P, SLOTS // 16], U16, name="offsets")
         ks_pool = keep.tile([P, TOKENS], U8, name="ks_pool", align_bytes=64)
         cs_pool = keep.tile([P, TOKENS], U8, name="cs_pool", align_bytes=64)
         ls_rows = keep.tile([P, P], F32, name="ls_rows")
         ident = keep.tile([P, P], F32, name="ident")
-        q_raw = keep.tile([P, PACK, NQ], F32, name="q_raw")
+        q_raw = [keep.tile([P, PACK, HALF], F32, name="q_raw%d" % g) for g in range(2)]
         k_pool = keep.tile([P, TOKENS], U32, name="k_pool", align_bytes=64)
-        planes = keep.tile([P, 2, SLOTS], U8, name="planes", align_bytes=64)
+        planes = [keep.tile([P, SLOTS], U8, name="plane%d" % table, align_bytes=64) for table in range(2)]
 
         nc.vector.memset(ks_pool[0:LOADED, :].bitcast(I32), 0)
         nc.vector.memset(cs_pool[0:LOADED, :].bitcast(I32), 0)
         nc.vector.memset(ident[:], 0.0)
         nc.vector.memset(ls_rows[0:P - QT, :], 0.0)
-        nc.vector.memset(planes[:].rearrange("p t n -> p (t n)").bitcast(I32), 0)
+        for plane in planes:
+            nc.vector.memset(plane[:].bitcast(I32), 0)
         make_identity(nc, ident[:], nomemset=True)
 
+        q_rows = qT[0].rearrange("(p j) w -> p j w", j=PACK)
         nc.sync.dma_start(offsets[:], offs)
         nc.scalar.dma_start(ks_pool[LOADED:P, :].bitcast(I32), k_scales[0].bitcast(I32))
-        nc.sync.dma_start(q_raw[:], qT[0].rearrange("(p j) w -> p j w", j=PACK))
+        nc.sync.dma_start(q_raw[0][:], q_rows[:, :, 0:HALF])
         nc.sync.dma_start(cs_pool[LOADED:P, :].bitcast(I32), c_scales[0].bitcast(I32))
         nc.sync.dma_start(ls_rows[P - QT:P, :], ls[0, 0].rearrange("(t p) -> t p", p=P))
         nc.sync.dma_start(k_pool[:].bitcast(I32), as_words(k_words))
+        nc.sync.dma_start(q_raw[1][:], q_rows[:, :, HALF:NQ])
 
         def to_plane(table, gathered):
             for j in range(ROWS):
-                nc.sync.dma_start(planes[j:P:QUAD, table, :].bitcast(I32), gathered[LOADED + j:P:ROWS, :].bitcast(I32))
+                nc.sync.dma_start(planes[table][j:P:QUAD, :].bitcast(I32), gathered[LOADED + j:P:ROWS, :].bitcast(I32))
 
-        ls_ps = psum.tile([P, P], F32, name="ls_ps", tag="bank%d" % (2 * QT - 1))
+        ls_ps = bank(7, "ls_ps", [P])
         nc.tensor.transpose(ls_ps[:], ls_rows[:], ident[:])
         neg_ls = keep.tile([P, QT], F32, name="neg_ls")
         nc.scalar.activation(neg_ls[:], ls_ps[:, P - QT:P], ACT.Copy, scale=-1.0)
@@ -83,129 +89,93 @@ def tile_attend_plw_cfg_topk_kernel(tc, qT, k_words, k_scales, c_words, c_scales
         nc.vector.tensor_copy(csg[:], cs_pool[:].indirect(offsets[:]))
         to_plane(1, csg)
 
-        q_bf = []
+        q_bf = [keep.tile([P, HALF, PACK], BF16, name="q_bf%d" % g, tag=("q_bf0", "k_pool")[g], align_bytes=64) for g in range(2)]
+        q_codes = keep.tile([P, NQ], U32, name="q_codes", tag="cs_pool", align_bytes=64)
+        q_scales = [keep.tile([P, HALF], U8, name="q_scales%d" % g, align_bytes=64) for g in range(2)]
+
+        def quantise_q(g, first, stop):
+            nc.vector.quantize_mx(out=q_codes[:, g * HALF + first:g * HALF + stop].bitcast(FP8X4), scales=q_scales[g][:, first:stop],
+                                  in_=q_bf[g][:, first:stop, :].rearrange("p w j -> p (w j)"))
+
+        nc.scalar.copy(*woven(q_bf[0][:], q_raw[0][:]))
+        quantise_q(0, 0, HALF)
+        nc.vector.tensor_copy(kg[:], k_pool[:].indirect(offsets[:]))
+        nc.vector.tensor_copy(*woven(q_bf[1][:, 0:P, :], q_raw[1][:, :, 0:P]))
+        nc.scalar.copy(*woven(q_bf[1][:, P:HALF, :], q_raw[1][:, :, P:HALF]))
+        quantise_q(1, 0, P)
+        quantise_q(1, P, HALF)
+
+        def scores(out, t, slots, words, table):
+            nc.tensor.matmul_mx(out=out, lhsT=q_codes[:, t * P:(t + 1) * P].bitcast(FP8X4),
+                                lhsT_scale=q_scales[t // 2][:, t % 2 * P:(t % 2 + 1) * P],
+                                rhs=words[:, slots].bitcast(FP8X4), rhs_scale=planes[table][:, slots], start=True, stop=True)
+
+        def dealt(scored):
+            return scored.rearrange("p (s r) -> p r s", r=PACK)
+
+        units = [((0, 2), (2, PACK))] + [((0, PACK),)] * (QT - 1)
+        u = [{unit: keep.tile([P, unit[1] - unit[0], P], F32, name="u%d_%d" % (t, unit[0]))[:] for unit in units[t]} for t in range(QT)]
+        for t in range(QT):
+            a = bank(t, "a%d" % t, [SLOTS])
+            scores(a[:], t, slice(0, SLOTS), kg, 0)
+            for first, stop in units[t]:
+                nc.scalar.activation(u[t][first, stop], dealt(a[:])[:, first:stop, :], ACT.Identity, bias=neg_ls[:, t:t + 1], scale=1.5)
+        w_late = keep.tile([P, 2, PACK, P], F32, name="w_late", tag="u0_0")
+        w = [keep.tile([P, PACK, P], F32, name="w%d" % t)[:] if t < 2 else w_late[:, t - 2, :, :] for t in range(QT)]
+
+        halves = [slice(0, HALF), slice(HALF, SLOTS)]
         for h in range(2):
-            rounded = keep.tile([P, HALF, PACK], BF16, name="q_bf%d" % h, align_bytes=64)
-            if h == 0:
-                nc.scalar.copy(*woven(rounded[:], q_raw[:, :, 0:HALF]))
-            else:
-                nc.scalar.copy(*woven(rounded[:, 0:P, :], q_raw[:, :, HALF:HALF + P]))
-                nc.vector.tensor_copy(*woven(rounded[:, P:HALF, :], q_raw[:, :, HALF + P:NQ]))
-            q_bf.append(rounded)
+            nc.vector.tensor_copy(cg[:, halves[h]], c_pool[:].indirect(offsets[:, h * (HALF // 16):(h + 1) * (HALF // 16)]))
 
-        q_codes, q_scales = [], []
-        all_codes = keep.tile([P, NQ], U32, name="q_codes", tag="cs_pool", align_bytes=64)
+        z = {}
+        for h, banks in enumerate(((4, 5, 6), (2, 3, 7))):
+            pair = bank(banks[2], "z_pair%d" % h, [2, HALF])
+            for t in range(QT):
+                z[h, t] = bank(banks[t], "z%d_%d" % (h, t), [HALF])[:] if t < 2 else pair[:, t - 2, :]
+                scores(z[h, t], t, halves[h], cg, 1)
 
-        def quantise_q(tiles, tag):
-            first, width = tiles.start * P, len(tiles) * P
-            scales = keep.tile([P, width], U8, name="q_scales%d" % tiles.start, tag=tag, align_bytes=64)
-            rounded = q_bf[first // HALF][:, first % HALF:first % HALF + width, :]
-            nc.vector.quantize_mx(out=all_codes[:, first:first + width].bitcast(FP8X4), scales=scales[:],
-                                  in_=rounded.rearrange("p w j -> p (w j)"))
-            for t in tiles:
-                q_codes.append(all_codes[:, t * P:(t + 1) * P])
-                q_scales.append(scales[:, t * P - first:(t + 1) * P - first])
+        def part(view, h):
+            return view[:, :, h * (P // 2):(h + 1) * (P // 2)]
 
-        def gather_words(dst, pool, h):
-            nc.vector.tensor_copy(dst[:, h * HALF:(h + 1) * HALF], pool[:].indirect(offsets[:, h * (HALF // 16):(h + 1) * (HALF // 16)]))
+        def exponent(h, t, first=0, stop=PACK):
+            nc.vector.scalar_tensor_tensor(part(w[t][:, first:stop, :], h), dealt(z[h, t])[:, first:stop, :], -0.5,
+                                           part(u[t][first, stop], h), ALU.mult, ALU.add)
 
-        quantise_q(range(0, 2), "q_scales0")
-        quantise_q(range(2, 3), "q_scales2")
-        gather_words(kg, k_pool, 0)
-        gather_words(kg, k_pool, 1)
-        quantise_q(range(QT - 1, QT), "k_pool")
-
-        def scores(out, t, h, words, table):
-            slots = slice(0, SLOTS) if h is None else slice(h * HALF, (h + 1) * HALF)
-            nc.tensor.matmul_mx(out=out, lhsT=q_codes[t].bitcast(FP8X4), lhsT_scale=q_scales[t],
-                                rhs=words[:, slots].bitcast(FP8X4), rhs_scale=planes[:, table, slots], start=True, stop=True)
-
-        def dealt(bank):
-            return bank.rearrange("p (s r) -> p r s", r=PACK)
-
-        a = [psum.tile([P, SLOTS], F32, name="a_ps%d" % t, tag="bank%d" % t) for t in range(QT - 1)]
-        u = [keep.tile([P, PACK, 2, P], F32, name="u%d" % g) for g in range(2)]
-        w = [keep.tile([P, PACK, 2, P], F32, name="w%d" % g) for g in range(2)]
-        for t in range(2):
-            scores(a[t][:, 0:HALF], t, 0, kg, 0)
-
-        def first_term(t):
-            if t < 2:
-                scores(a[t][:, HALF:SLOTS], t, 1, kg, 0)
-            else:
-                scores(a[t][:], t, None, kg, 0)
-            nc.scalar.activation(u[t // 2][:, :, t % 2, :], dealt(a[t][:]), ACT.Identity, bias=neg_ls[:, t:t + 1], scale=1.5)
-
-        for t in range(QT - 1):
-            first_term(t)
-        gather_words(cg, c_pool, 0)
-        gather_words(cg, c_pool, 1)
-
-        y_rows = out_0.rearrange("(p r) q -> p r q", r=PACK)
-        y_words = as_words(out_1)
-        y_codes = keep.tile([P, NQ], U32, name="y_codes", align_bytes=64)
-        y_scales = keep.tile([P, NQ], U8, name="y_scales", align_bytes=64)
-
-        def half_of(pair, h):
-            return pair[:].rearrange("p r t (h s) -> p (r t) h s", h=2)[:, :, h, :]
-
-        z_first = [psum.tile([P, HALF], F32, name="z_first%d" % t, tag="bank%d" % (0, QT)[t]) for t in range(2)]
-        z_second = psum.tile([P, 2, HALF], F32, name="z_second", tag="bank%d" % (QT + 1))
-        z_tile = [psum.tile([P, SLOTS], F32, name="z_tile%d" % t, tag="bank%d" % (QT + 2 + t)) for t in range(2)]
-
-        def last_first_term(h, bank):
-            part = psum.tile([P, HALF], F32, name="a_last%d" % h, tag="bank%d" % bank)
-            scores(part[:], QT - 1, h, kg, 0)
-            nc.scalar.activation(u[1][:, :, 1, h * (P // 2):(h + 1) * (P // 2)], dealt(part[:]), ACT.Identity, bias=neg_ls[:, QT - 1:QT], scale=1.5)
-
-        last_first_term(0, QT - 1)
-        for t in range(2):
-            scores(z_first[t][:], t, 0, cg, 1)
-        for t in range(2):
-            scores(z_second[:, t, :], t, 1, cg, 1)
-        for t in range(2):
-            scores(z_tile[t][:], 2 + t, None, cg, 1)
-
-        def exponent(out, z, u_part):
-            nc.vector.scalar_tensor_tensor(out, dealt(z), -0.5, u_part, ALU.mult, ALU.add)
-
-        for t in range(2):
-            exponent(w[0][:, :, t, 0:P // 2], z_first[t][:], u[0][:, :, t, 0:P // 2])
-        last_first_term(1, 0)
-        for first, stop in ((0, 1), (1, 2), (2, PACK)):
-            nc.vector.scalar_tensor_tensor(half_of(w[0], 1)[:, 2 * first:2 * stop, :],
-                                           dealt(z_second[:].rearrange("p t n -> p (t n)"))[:, first:stop, :], -0.5,
-                                           half_of(u[0], 1)[:, 2 * first:2 * stop, :], ALU.mult, ALU.add)
-        exponent(w[1][:, :, 0, :], z_tile[0][:], u[1][:, :, 0, :])
-        for first in (0, 2):
-            nc.vector.scalar_tensor_tensor(w[1][:, first:first + 2, 1, :], dealt(z_tile[1][:])[:, first:first + 2, :], -0.5,
-                                           u[1][:, first:first + 2, 1, :], ALU.mult, ALU.add)
+        for h in range(2):
+            nc.scalar.activation(part(w[1], h), dealt(z[h, 1]), ACT.Copy, scale=-0.5)
+        for first, stop in units[0]:
+            for h in range(2):
+                exponent(h, 0, first, stop)
+        for t in range(2, QT):
+            for h in range(2):
+                exponent(h, t)
 
         y = keep.tile([P, PACK, NQ], F32, name="y")
         y_bf = keep.tile([P, NQ, PACK], BF16, name="y_bf", align_bytes=64)
+        y_rows = out_0.rearrange("(p r) q -> p r q", r=PACK)
+        y_codes = keep.tile([P, NQ], U32, name="y_codes", align_bytes=64)
+        y_scales = keep.tile([P, NQ], U8, name="y_scales", align_bytes=64)
 
-        def finish(bank, places, tiles):
-            turned = psum.tile([P, len(places), len(tiles), P], F32, name="turned%d" % bank, tag="bank%d" % bank)
-            for r in places:
-                for t in tiles:
-                    nc.tensor.transpose(turned[:, r - places.start, t - tiles.start, :], w[t // 2][:, r, t % 2, :], ident[:])
-            rows, cols = slice(places.start, places.stop), slice(tiles.start * P, tiles.stop * P)
-            nc.scalar.activation(y[:, rows, cols], turned[:].rearrange("p r t q -> p r (t q)"), ACT.Exp)
-
-        finish(QT, range(0, 1), range(0, 2))
-        finish(QT - 1, range(1, 2), range(0, 2))
-        nc.sync.dma_start(y_rows[:, 0:2, 0:HALF], y[:, 0:2, 0:HALF])
-        finish(1, range(2, PACK), range(0, 2))
-        nc.sync.dma_start(y_rows[:, 2:PACK, 0:HALF], y[:, 2:PACK, 0:HALF])
-        turned = [psum.tile([P, PACK, P], F32, name="turned_tile%d" % t, tag="bank%d" % (2, QT + 1)[t]) for t in range(2)]
+        for g in range(2):
+            turned = bank((4, 0)[g], "turned0_%d" % g, [2, P])
+            for r in range(2):
+                nc.tensor.transpose(turned[:, r, :], w[0][:, 2 * g + r, :], ident[:])
+            nc.scalar.activation(y[:, 2 * g:2 * g + 2, 0:P], turned[:], ACT.Exp)
+            summed = bank((5, 3)[g], "summed%d" % g, [2, P])
+            for n, term in enumerate((u[1][0, PACK], w[1])):
+                for r in range(2):
+                    nc.tensor.matmul(summed[:, r, :], term[:, 2 * g + r, :], ident[:], start=(n, r) == (0, 0),
+                                     stop=(n, r) == (1, 1), is_transpose=True)
+            nc.scalar.activation(y[:, 2 * g:2 * g + 2, P:HALF], summed[:], ACT.Exp)
+            nc.sync.dma_start(y_rows[:, 2 * g:2 * g + 2, 0:HALF], y[:, 2 * g:2 * g + 2, 0:HALF])
+        turned = [bank((2, 1)[t], "turned%d" % (2 + t), [PACK, P]) for t in range(2)]
         for t in range(2):
             for r in range(PACK):
-                nc.tensor.transpose(turned[t][:, r, :], w[1][:, r, t, :], ident[:])
+                nc.tensor.transpose(turned[t][:, r, :], w[2 + t][:, r, :], ident[:])
         nc.scalar.activation(y[:, :, HALF:HALF + P], turned[0][:], ACT.Exp)
         for first in (0, 2):
             nc.scalar.activation(y[:, first:first + 2, NQ - P:NQ], turned[1][:, first:first + 2, :], ACT.Exp)
             nc.sync.dma_start(y_rows[:, first:first + 2, HALF:NQ], y[:, first:first + 2, HALF:NQ])
-        nc.scalar.activation(y_bf[:, NQ - P:NQ, :], turned[1][:].rearrange("p r q -> p q r"), ACT.Exp)
 
         def round_y(first, stop):
             nc.vector.tensor_copy(*woven(y_bf[:, first:stop, :], y[:, :, first:stop]))
@@ -214,12 +184,14 @@ def tile_attend_plw_cfg_topk_kernel(tc, qT, k_words, k_scales, c_words, c_scales
             nc.vector.quantize_mx(out=y_codes[:, first:stop].bitcast(FP8X4), scales=y_scales[:, first:stop],
                                   in_=y_bf[:, first:stop, :].rearrange("p w j -> p (w j)"))
 
-        round_y(0, HALF)
+        nc.scalar.activation(y_bf[:, NQ - P:NQ, :], turned[1][:].rearrange("p r q -> p q r"), ACT.Exp)
+        round_y(0, P)
+        round_y(P, HALF)
         round_y(HALF, HALF + P)
         quantise_y(0, HALF)
         quantise_y(HALF, HALF + P)
         quantise_y(NQ - P, NQ)
-        nc.sync.dma_start(y_words, y_codes[:].bitcast(I32))
+        nc.sync.dma_start(as_words(out_1), y_codes[:].bitcast(I32))
         for j in range(ROWS):
             queue = nc.sync if j == 0 else nc.scalar
             queue.dma_start(out_2[0, j:ROWS * ROWS:ROWS, :].bitcast(I32), y_scales[j:P:QUAD, :].bitcast(I32))

@@ -52,8 +52,8 @@ def tile_attend_plw_cfg_topk_kernel(tc, qT, k_words, k_scales, c_words, c_scales
         k_pool = keep.tile([P, TOKENS], U32, name="k_pool", align_bytes=64)
         planes = [keep.tile([P, SLOTS], U8, name="plane%d" % table, align_bytes=64) for table in range(2)]
 
+        nc.vector.memset(cs_pool[:].bitcast(I32), 0)
         nc.vector.memset(ks_pool[0:LOADED, :].bitcast(I32), 0)
-        nc.vector.memset(cs_pool[0:LOADED, :].bitcast(I32), 0)
         nc.vector.memset(ident[:], 0.0)
         nc.vector.memset(ls_rows[0:P - QT, :], 0.0)
         for plane in planes:
@@ -64,14 +64,14 @@ def tile_attend_plw_cfg_topk_kernel(tc, qT, k_words, k_scales, c_words, c_scales
         nc.sync.dma_start(offsets[:], offs)
         nc.scalar.dma_start(ks_pool[LOADED:P, :].bitcast(I32), k_scales[0].bitcast(I32))
         nc.sync.dma_start(q_raw[0][:], q_rows[:, :, 0:HALF])
-        nc.sync.dma_start(cs_pool[LOADED:P, :].bitcast(I32), c_scales[0].bitcast(I32))
+        nc.sync.dma_start(cs_pool[QUAD:P - QUAD:ROWS, :].bitcast(I32), c_scales[0].bitcast(I32))
         nc.sync.dma_start(ls_rows[P - QT:P, :], ls[0, 0].rearrange("(t p) -> t p", p=P))
         nc.sync.dma_start(k_pool[:].bitcast(I32), as_words(k_words))
         nc.sync.dma_start(q_raw[1][:], q_rows[:, :, HALF:NQ])
 
-        def to_plane(table, gathered):
+        def to_plane(table, gathered, first, step):
             for j in range(ROWS):
-                nc.sync.dma_start(planes[table][j:P:QUAD, :].bitcast(I32), gathered[LOADED + j:P:ROWS, :].bitcast(I32))
+                nc.sync.dma_start(planes[table][j:P:QUAD, :].bitcast(I32), gathered[first + step * j:first + step * BLOCKS:step * ROWS, :].bitcast(I32))
 
         ls_ps = bank(7, "ls_ps", [P])
         nc.tensor.transpose(ls_ps[:], ls_rows[:], ident[:])
@@ -83,11 +83,11 @@ def tile_attend_plw_cfg_topk_kernel(tc, qT, k_words, k_scales, c_words, c_scales
         cg = keep.tile([P, SLOTS], U32, name="cg", align_bytes=64)
         csg = keep.tile([P, SLOTS], U8, name="csg", align_bytes=64)
         nc.vector.tensor_copy(ksg[:], ks_pool[:].indirect(offsets[:]))
-        to_plane(0, ksg)
+        to_plane(0, ksg, LOADED, 1)
         c_pool = keep.tile([P, TOKENS], U32, name="c_pool", tag="ks_pool", align_bytes=64)
         nc.sync.dma_start(c_pool[:].bitcast(I32), as_words(c_words))
         nc.vector.tensor_copy(csg[:], cs_pool[:].indirect(offsets[:]))
-        to_plane(1, csg)
+        to_plane(1, csg, QUAD, ROWS)
 
         q_bf = [keep.tile([P, HALF, PACK], BF16, name="q_bf%d" % g, tag=("q_bf0", "k_pool")[g], align_bytes=64) for g in range(2)]
         q_codes = keep.tile([P, NQ], U32, name="q_codes", tag="cs_pool", align_bytes=64)

from contextlib import ExitStack

import concourse.mybir as mybir
from concourse.masks import make_identity

F32 = mybir.dt.float32
BF16 = mybir.dt.bfloat16
I32 = mybir.dt.int32
U32 = mybir.dt.uint32
U16 = mybir.dt.uint16
U8 = mybir.dt.uint8
FP8X4 = mybir.dt.float8_e4m3fn_x4
ALU = mybir.AluOpType
ACT = mybir.ActivationFunctionType

P = 128
PACK = 4
QUAD = 32
ROWS = 4
SLOTS, TOKENS, D, NQ = 512, 2048, 512, 512
QT = NQ // P
HALF = 256
BLOCKS = D // 32
LOADED = P - BLOCKS
LINE = 4

FLOPS = 2 * 2 * SLOTS * D * NQ


def tile_attend_plw_cfg_topk_kernel(tc, qT, k_words, k_scales, c_words, c_scales, ls, offs, out_0, out_1, out_2):
    nc = tc.nc

    def woven(dst, src):
        return dst.rearrange("p (c i) t -> p c t i", i=LINE), src.rearrange("p t (c i) -> p c t i", i=LINE)

    def as_words(packed):
        return packed[0].rearrange("p n t -> p (n t)").bitcast(I32)

    with ExitStack() as ctx:
        keep = ctx.enter_context(tc.tile_pool(name="keep", bufs=1))
        psum = ctx.enter_context(tc.psum_pool(name="psum", bufs=1))

        def bank(number, name, shape):
            return psum.tile([P] + shape, F32, name=name, tag="bank%d" % number)

        offsets = keep.tile([P, SLOTS // 16], U16, name="offsets")
        ks_pool = keep.tile([P, TOKENS], U8, name="ks_pool", align_bytes=64)
        cs_pool = keep.tile([P, TOKENS], U8, name="cs_pool", align_bytes=64)
        ls_rows = keep.tile([P, P], F32, name="ls_rows")
        ident = keep.tile([P, P], F32, name="ident")
        q_raw = [keep.tile([P, PACK, HALF], F32, name="q_raw%d" % g) for g in range(2)]
        k_pool = keep.tile([P, TOKENS], U32, name="k_pool", align_bytes=64)
        planes = [keep.tile([P, SLOTS], U8, name="plane%d" % table, align_bytes=64) for table in range(2)]

        nc.vector.memset(cs_pool[:].bitcast(I32), 0)
        nc.vector.memset(ks_pool[0:LOADED, :].bitcast(I32), 0)
        nc.vector.memset(ident[:], 0.0)
        nc.vector.memset(ls_rows[0:P - QT, :], 0.0)
        for plane in planes:
            nc.vector.memset(plane[:].bitcast(I32), 0)
        make_identity(nc, ident[:], nomemset=True)

        q_rows = qT[0].rearrange("(p j) w -> p j w", j=PACK)
        nc.sync.dma_start(offsets[:], offs)
        nc.scalar.dma_start(ks_pool[LOADED:P, :].bitcast(I32), k_scales[0].bitcast(I32))
        nc.sync.dma_start(q_raw[0][:], q_rows[:, :, 0:HALF])
        nc.sync.dma_start(cs_pool[QUAD:P - QUAD:ROWS, :].bitcast(I32), c_scales[0].bitcast(I32))
        nc.sync.dma_start(ls_rows[P - QT:P, :], ls[0, 0].rearrange("(t p) -> t p", p=P))
        nc.sync.dma_start(k_pool[:].bitcast(I32), as_words(k_words))
        nc.sync.dma_start(q_raw[1][:], q_rows[:, :, HALF:NQ])

        def to_plane(table, gathered, first, step):
            for j in range(ROWS):
                nc.sync.dma_start(planes[table][j:P:QUAD, :].bitcast(I32), gathered[first + step * j:first + step * BLOCKS:step * ROWS, :].bitcast(I32))

        ls_ps = bank(7, "ls_ps", [P])
        nc.tensor.transpose(ls_ps[:], ls_rows[:], ident[:])
        neg_ls = keep.tile([P, QT], F32, name="neg_ls")
        nc.scalar.activation(neg_ls[:], ls_ps[:, P - QT:P], ACT.Copy, scale=-1.0)

        ksg = keep.tile([P, SLOTS], U8, name="ksg", align_bytes=64)
        kg = keep.tile([P, SLOTS], U32, name="kg", align_bytes=64)
        cg = keep.tile([P, SLOTS], U32, name="cg", align_bytes=64)
        csg = keep.tile([P, SLOTS], U8, name="csg", align_bytes=64)
        nc.vector.tensor_copy(ksg[:], ks_pool[:].indirect(offsets[:]))
        to_plane(0, ksg, LOADED, 1)
        c_pool = keep.tile([P, TOKENS], U32, name="c_pool", tag="ks_pool", align_bytes=64)
        nc.sync.dma_start(c_pool[:].bitcast(I32), as_words(c_words))
        nc.vector.tensor_copy(csg[:], cs_pool[:].indirect(offsets[:]))
        to_plane(1, csg, QUAD, ROWS)

        q_bf = [keep.tile([P, HALF, PACK], BF16, name="q_bf%d" % g, tag=("q_bf0", "k_pool")[g], align_bytes=64) for g in range(2)]
        q_codes = keep.tile([P, NQ], U32, name="q_codes", tag="cs_pool", align_bytes=64)
        q_scales = [keep.tile([P, HALF], U8, name="q_scales%d" % g, align_bytes=64) for g in range(2)]

        def quantise_q(g, first, stop):
            nc.vector.quantize_mx(out=q_codes[:, g * HALF + first:g * HALF + stop].bitcast(FP8X4), scales=q_scales[g][:, first:stop],
                                  in_=q_bf[g][:, first:stop, :].rearrange("p w j -> p (w j)"))

        nc.scalar.copy(*woven(q_bf[0][:], q_raw[0][:]))
        quantise_q(0, 0, HALF)
        nc.vector.tensor_copy(kg[:], k_pool[:].indirect(offsets[:]))
        nc.vector.tensor_copy(*woven(q_bf[1][:, 0:P, :], q_raw[1][:, :, 0:P]))
        nc.scalar.copy(*woven(q_bf[1][:, P:HALF, :], q_raw[1][:, :, P:HALF]))
        quantise_q(1, 0, P)
        quantise_q(1, P, HALF)

        def scores(out, t, slots, words, table):
            nc.tensor.matmul_mx(out=out, lhsT=q_codes[:, t * P:(t + 1) * P].bitcast(FP8X4),
                                lhsT_scale=q_scales[t // 2][:, t % 2 * P:(t % 2 + 1) * P],
                                rhs=words[:, slots].bitcast(FP8X4), rhs_scale=planes[table][:, slots], start=True, stop=True)

        def dealt(scored):
            return scored.rearrange("p (s r) -> p r s", r=PACK)

        units = [((0, 2), (2, PACK))] + [((0, PACK),)] * (QT - 1)
        u = [{unit: keep.tile([P, unit[1] - unit[0], P], F32, name="u%d_%d" % (t, unit[0]))[:] for unit in units[t]} for t in range(QT)]
        for t in range(QT):
            a = bank(t, "a%d" % t, [SLOTS])
            scores(a[:], t, slice(0, SLOTS), kg, 0)
            for first, stop in units[t]:
                nc.scalar.activation(u[t][first, stop], dealt(a[:])[:, first:stop, :], ACT.Identity, bias=neg_ls[:, t:t + 1], scale=1.5)
        w_late = keep.tile([P, 2, PACK, P], F32, name="w_late", tag="u0_0")
        w = [keep.tile([P, PACK, P], F32, name="w%d" % t)[:] if t < 2 else w_late[:, t - 2, :, :] for t in range(QT)]

        halves = [slice(0, HALF), slice(HALF, SLOTS)]
        for h in range(2):
            nc.vector.tensor_copy(cg[:, halves[h]], c_pool[:].indirect(offsets[:, h * (HALF // 16):(h + 1) * (HALF // 16)]))

        z = {}
        for h, banks in enumerate(((4, 5, 6), (2, 3, 7))):
            pair = bank(banks[2], "z_pair%d" % h, [2, HALF])
            for t in range(QT):
                z[h, t] = bank(banks[t], "z%d_%d" % (h, t), [HALF])[:] if t < 2 else pair[:, t - 2, :]
                scores(z[h, t], t, halves[h], cg, 1)

        def part(view, h):
            return view[:, :, h * (P // 2):(h + 1) * (P // 2)]

        def exponent(h, t, first=0, stop=PACK):
            nc.vector.scalar_tensor_tensor(part(w[t][:, first:stop, :], h), dealt(z[h, t])[:, first:stop, :], -0.5,
                                           part(u[t][first, stop], h), ALU.mult, ALU.add)

        for h in range(2):
            nc.scalar.activation(part(w[1], h), dealt(z[h, 1]), ACT.Copy, scale=-0.5)
        for first, stop in units[0]:
            for h in range(2):
                exponent(h, 0, first, stop)
        for t in range(2, QT):
            for h in range(2):
                exponent(h, t)

        y = keep.tile([P, PACK, NQ], F32, name="y")
        y_bf = keep.tile([P, NQ, PACK], BF16, name="y_bf", align_bytes=64)
        y_rows = out_0.rearrange("(p r) q -> p r q", r=PACK)
        y_codes = keep.tile([P, NQ], U32, name="y_codes", align_bytes=64)
        y_scales = keep.tile([P, NQ], U8, name="y_scales", align_bytes=64)

        for g in range(2):
            turned = bank((4, 0)[g], "turned0_%d" % g, [2, P])
            for r in range(2):
                nc.tensor.transpose(turned[:, r, :], w[0][:, 2 * g + r, :], ident[:])
            nc.scalar.activation(y[:, 2 * g:2 * g + 2, 0:P], turned[:], ACT.Exp)
            summed = bank((5, 3)[g], "summed%d" % g, [2, P])
            for n, term in enumerate((u[1][0, PACK], w[1])):
                for r in range(2):
                    nc.tensor.matmul(summed[:, r, :], term[:, 2 * g + r, :], ident[:], start=(n, r) == (0, 0),
                                     stop=(n, r) == (1, 1), is_transpose=True)
            nc.scalar.activation(y[:, 2 * g:2 * g + 2, P:HALF], summed[:], ACT.Exp)
            nc.sync.dma_start(y_rows[:, 2 * g:2 * g + 2, 0:HALF], y[:, 2 * g:2 * g + 2, 0:HALF])
        turned = [bank((2, 1)[t], "turned%d" % (2 + t), [PACK, P]) for t in range(2)]
        for t in range(2):
            for r in range(PACK):
                nc.tensor.transpose(turned[t][:, r, :], w[2 + t][:, r, :], ident[:])
        nc.scalar.activation(y[:, :, HALF:HALF + P], turned[0][:], ACT.Exp)
        for first in (0, 2):
            nc.scalar.activation(y[:, first:first + 2, NQ - P:NQ], turned[1][:, first:first + 2, :], ACT.Exp)
            nc.sync.dma_start(y_rows[:, first:first + 2, HALF:NQ], y[:, first:first + 2, HALF:NQ])

        def round_y(first, stop):
            nc.vector.tensor_copy(*woven(y_bf[:, first:stop, :], y[:, :, first:stop]))

        def quantise_y(first, stop):
            nc.vector.quantize_mx(out=y_codes[:, first:stop].bitcast(FP8X4), scales=y_scales[:, first:stop],
                                  in_=y_bf[:, first:stop, :].rearrange("p w j -> p (w j)"))

        nc.scalar.activation(y_bf[:, NQ - P:NQ, :], turned[1][:].rearrange("p r q -> p q r"), ACT.Exp)
        round_y(0, P)
        round_y(P, HALF)
        round_y(HALF, HALF + P)
        quantise_y(0, HALF)
        quantise_y(HALF, HALF + P)
        quantise_y(NQ - P, NQ)
        nc.sync.dma_start(as_words(out_1), y_codes[:].bitcast(I32))
        for j in range(ROWS):
            queue = nc.sync if j == 0 else nc.scalar
            queue.dma_start(out_2[0, j:ROWS * ROWS:ROWS, :].bitcast(I32), y_scales[j:P:QUAD, :].bitcast(I32))
